import numpy as np
import ml_dtypes


def mxq(x, axis, fmt="e4m3"):
    dtype, down = {"e4m3": (ml_dtypes.float8_e4m3fn, 7), "e5m2": (ml_dtypes.float8_e5m2, 14)}[fmt]
    v = np.moveaxis(np.asarray(x, np.float32).astype(ml_dtypes.bfloat16).astype(np.float64), axis, -1)
    blocks = v.reshape(v.shape[:-1] + (-1, 32))
    amax = np.abs(blocks).max(-1, keepdims=True)
    byte = np.maximum(np.where(amax > 0, np.frexp(amax)[1] - 1 + 127, 0) - down, 1)
    scale = np.exp2(byte - 127.0)
    codes = (blocks / scale).astype(np.float32).astype(dtype).astype(np.float64)
    return np.moveaxis((codes * scale).reshape(v.shape), -1, axis)


WIDE = False


def mx_kscale(k):
    if not WIDE:
        return np.ones(k)
    levels = np.array([10, -10, 5, -5, 0])
    if k % 512:
        return np.exp2(np.random.permutation(np.resize(levels, k // 32))).repeat(32)
    a = np.empty((k // 512, 16))
    for p in range(k // 512):
        a[p, :8] = np.random.permutation(np.resize(levels, 8))
        for g in range(8):
            far = levels[np.abs(levels - a[p, g]) >= 10]
            a[p, g + 8] = far[np.random.randint(len(far))]
    return np.exp2(a.ravel()).repeat(32)


def f64(x):
    return np.asarray(x).astype(np.float64)


def striped(idx):
    return np.tile(idx.reshape(-1, 16).T, (8, 1)).astype(np.uint16)


def unstriped(offs):
    return offs[:16].T.reshape(-1).astype(np.int64)


def pack_weight(w):
    k, n = w.shape
    w = f64(np.asarray(w, np.float32).astype(ml_dtypes.bfloat16)).reshape(k // 32, 32, n)
    amax = np.abs(w).max(1)
    byte = np.clip(np.where(amax > 0, np.frexp(amax)[1] - 1 + 127 - 7, 1), 1, 254)
    scaled = (w * np.exp2(127.0 - byte)[:, None, :]).reshape(k, n).astype(np.float32)
    words = np.ascontiguousarray(scaled.reshape(k // 512, 128, 4, n).transpose(0, 1, 3, 2)).astype(ml_dtypes.float8_e4m3fn).view(np.uint8)
    return words, np.ascontiguousarray(byte.astype(np.uint8).reshape(k // 512, 16, n))


def unpack_weight(words, scales):
    g, p, n, _ = words.shape
    vals = np.ascontiguousarray(words).view(ml_dtypes.float8_e4m3fn).astype(np.float64) * np.repeat(np.exp2(scales.astype(np.float64) - 127.0), 8, axis=1)[..., None]
    return vals.transpose(0, 1, 3, 2).reshape(g * 512, n)

def planes(y):
    n, m = y.shape
    v = y.astype(np.float32).astype(ml_dtypes.bfloat16).astype(np.float64).reshape(n // 32, 32, m)
    top = np.abs(v).max(1)
    byte = np.clip(np.where(top > 0, np.frexp(top)[1] - 1 + 127 - 7, 1), 1, 254)
    codes = (v * np.exp2(127.0 - byte)[:, None, :]).reshape(n, m).astype(np.float32).astype(ml_dtypes.float8_e4m3fn).view(np.uint8)
    words = codes.reshape(n // 512, 128, 4, m).transpose(0, 1, 3, 2)
    return np.ascontiguousarray(words), np.ascontiguousarray(byte.astype(np.uint8).reshape(n // 512, 16, m))


K, T, S, V, H = 512, 1024, 512, 256, 512


def setup_inputs():
    n = np.random.standard_normal
    s = mx_kscale(K)[:, None]
    u = mx_kscale(H)
    packed_xT = pack_weight(n((K, T)) * s)
    packed_w2 = pack_weight(n((H, H)) / np.sqrt(3 * H) / u[:, None])
    packed_w3 = pack_weight(n((H, H)) / np.sqrt(3 * H) / u[:, None])
    packed_w4 = pack_weight(n((H, H)) / np.sqrt(3 * H) / u[:, None])
    return {
        "x_words": packed_xT[0],
        "x_scales": packed_xT[1],
        "w1": (n((K, H)) / np.sqrt(K) / s * u).astype(np.float32),
        "w2_words": packed_w2[0],
        "w2_scales": packed_w2[1],
        "w3_words": packed_w3[0],
        "w3_scales": packed_w3[1],
        "w4_words": packed_w4[0],
        "w4_scales": packed_w4[1],
        "offs": striped(np.random.permutation(T)[:S]),
        "pos1": striped(np.random.permutation(S)[:V]),
        "pos2": striped(np.random.permutation(S)[:V]),
        "pos3": striped(np.random.permutation(S)[:V]),
    }


def reference(x_words, x_scales, w1, w2_words, w2_scales, w3_words, w3_scales, w4_words, w4_scales, offs, pos1, pos2, pos3):
    xq = unpack_weight(x_words, x_scales)[:, unstriped(offs)]
    h = mxq(f64(w1), 0, "e4m3").T @ xq
    g0 = h[:, unstriped(pos1)]
    g1 = h[:, unstriped(pos2)]
    g2 = h[:, unstriped(pos3)]
    z1 = (g0 + g1 + g2) / 3
    z2 = np.maximum(np.maximum(g0, g1), g2)
    z3 = np.minimum(np.minimum(g0, g1), g2)
    out_0 = unpack_weight(w2_words, w2_scales).T @ mxq(z1, 0, "e4m3") + unpack_weight(w3_words, w3_scales).T @ mxq(z2, 0, "e4m3") + unpack_weight(w4_words, w4_scales).T @ mxq(z3, 0, "e4m3")
    return (out_0,) + planes(out_0)

@@ -1,0 +1,263 @@
+from contextlib import ExitStack
+
+import concourse.mybir as mybir
+from concourse.masks import make_identity
+
+K, T, S, V, H = 512, 1024, 512, 256, 512
+FLOPS = 2 * K * H * S + 3 * 2 * H * H * V
+
+F32 = mybir.dt.float32
+BF16 = mybir.dt.bfloat16
+I32 = mybir.dt.int32
+U32 = mybir.dt.uint32
+U16 = mybir.dt.uint16
+U8 = mybir.dt.uint8
+FP8X4 = mybir.dt.float8_e4m3fn_x4
+ALU = mybir.AluOpType
+COPY = mybir.ActivationFunctionType.Copy
+
+P = 128
+PACK = 4
+HALF = V // 2
+LINE = 4
+M_HALF = P // 2
+M_VECTOR = 40
+
+
+def as_words(words):
+    return words[0].rearrange("p n r -> p (n r)").bitcast(I32)
+
+
+def load_scale_rows(queue, plane, first_row, scales, quadrants=range(4)):
+    for q in quadrants:
+        row = 32 * q + first_row
+        queue.dma_start(out=plane[row : row + 4, :].bitcast(I32), in_=scales[0, 4 * q : 4 * q + 4, :].bitcast(I32))
+
+
+def tile_picked_pna_none_po_kernel(
+    tc, x_words, x_scales, w1, w2_words, w2_scales, w3_words, w3_scales, w4_words, w4_scales,
+    offs, pos1, pos2, pos3, out_0, out_1, out_2,
+):
+    nc = tc.nc
+    with ExitStack() as ctx:
+        sb = ctx.enter_context(tc.tile_pool(name="sb", bufs=1))
+        ps = ctx.enter_context(tc.psum_pool(name="ps", bufs=1))
+
+        def tile(name, shape, dtype, tag=""):
+            return sb.tile(shape, dtype, name=name, tag=tag or name, align_bytes=64)
+
+        def bank(number, name):
+            return ps.tile([P, 512], F32, name=name, tag="bank%d" % number)
+
+        offs_sb = tile("offs_sb", [P, S // 16], U16)
+        pos_sb = [tile("pos_sb%d" % d, [P, V // 16], U16) for d in range(3)]
+        x_plane = tile("x_plane", [P, T], U8)
+        x_codes = tile("x_codes", [P, T], U32)
+        w1_raw = [tile("w1_raw%d" % a, [P, PACK, H // 2], F32) for a in range(2)]
+        w_codes = [tile("w_codes%d" % d, [P, H], U32) for d in range(3)]
+        w_plane = tile("w_plane", [P, H], U8)
+        identity = tile("identity", [P, P], F32)
+
+        nc.vector.memset(x_plane[:].bitcast(I32), 0)
+        nc.vector.memset(w_plane[:].bitcast(I32), 0)
+        make_identity(nc, identity[:])
+
+        w1_rows = w1.rearrange("(p j) c -> p j c", j=PACK)
+        words_in = (w2_words, w3_words, w4_words)
+        nc.sync.dma_start(out=offs_sb[:], in_=offs)
+        nc.sync.dma_start(out=x_codes[:].bitcast(I32), in_=as_words(x_words))
+        nc.sync.dma_start(out=pos_sb[0][:], in_=pos1)
+        load_scale_rows(nc.sync, x_plane, 0, x_scales)
+        nc.sync.dma_start(out=w1_raw[0][:], in_=w1_rows[:, :, 0 : H // 2])
+        nc.sync.dma_start(out=w1_raw[1][:], in_=w1_rows[:, :, H // 2 : H])
+        nc.sync.dma_start(out=pos_sb[1][:], in_=pos2)
+        nc.sync.dma_start(out=pos_sb[2][:], in_=pos3)
+        for d in range(3):
+            nc.sync.dma_start(out=w_codes[d][:].bitcast(I32), in_=as_words(words_in[d]))
+        for d, scales in enumerate((w2_scales, w3_scales, w4_scales)):
+            load_scale_rows(nc.sync, w_plane, 4 * d, scales)
+
+        xp_plane = tile("xp_plane", [P, S], U8)
+        xp_codes = tile("xp_codes", [P, S], U32)
+        nc.vector.tensor_copy(out=xp_codes[:], in_=x_codes[:].indirect(offs_sb[:]))
+        nc.vector.tensor_copy(out=xp_plane[:], in_=x_plane[:].indirect(offs_sb[:]))
+
+        w1_bf = tile("w1_bf", [P, PACK, P, PACK], BF16)
+
+        def w1_views(a, m0, m1):
+            dst = w1_bf[:, :, M_HALF * a + m0 : M_HALF * a + m1, :].rearrange("p t m j -> p m t j")
+            src = w1_raw[a][:, :, PACK * m0 : PACK * m1].rearrange("p j (m t) -> p m t j", t=PACK)
+            return dst, src
+
+        dst, src = w1_views(0, 0, M_HALF)
+        nc.scalar.activation(out=dst, in_=src, func=COPY)
+        dst, src = w1_views(1, 0, M_VECTOR)
+        nc.vector.tensor_copy(out=dst, in_=src)
+        dst, src = w1_views(1, M_VECTOR, M_HALF)
+        nc.scalar.copy(out=dst, in_=src)
+
+        w1_codes = tile("w1_codes", [P, H], U32)
+        w1_plane = tile("w1_plane", [P, H], U8)
+        h = [tile("h%d" % t, [P, S], F32) for t in range(PACK)]
+        for t in range(PACK):
+            cols = slice(P * t, P * (t + 1))
+            nc.vector.quantize_mx(
+                out=w1_codes[:, cols].bitcast(FP8X4),
+                scales=w1_plane[:, cols],
+                in_=w1_bf[:, t].rearrange("p m j -> p (m j)"),
+            )
+
+        def first_product(t, number, first, count, copy):
+            cols = slice(P * t, P * (t + 1))
+            picked = slice(first, first + count)
+            acc = bank(number, "h_acc%d_%d" % (t, first))
+            nc.tensor.matmul_mx(
+                out=acc[:, 0:count],
+                lhsT=w1_codes[:, cols].bitcast(FP8X4),
+                lhsT_scale=w1_plane[:, cols],
+                rhs=xp_codes[:, picked].bitcast(FP8X4),
+                rhs_scale=xp_plane[:, picked],
+                start=True,
+                stop=True,
+            )
+            copy(out=h[t][:, picked], in_=acc[:, 0:count])
+
+        first_product(0, 0, 0, S // 2, nc.scalar.copy)
+        first_product(0, 7, S // 2, S // 2, nc.vector.tensor_copy)
+        for t in range(1, PACK):
+            first_product(t, t, 0, S, nc.scalar.copy)
+
+        wd_codes = [tile("wd_codes%d" % d, [P, H], U32) for d in range(3)]
+        wd_plane = tile("wd_plane", [P, H], U8)
+        y_codes = tile("y_codes", [P, V], U32)
+        y_plane = tile("y_plane", [P, V], U8)
+        out_rows = out_0.rearrange("(p t) v -> p t v", t=PACK)
+        out_words = as_words(out_1)
+        ops = {1: ALU.max, 2: ALU.min}
+        order = (1, 2, 0)
+
+        def deal():
+            for d in range(3):
+                nc.vector.tensor_copy(
+                    out=wd_codes[d][:].bitcast(I32).rearrange("p (t c i) -> p c t i", t=PACK, i=LINE),
+                    in_=w_codes[d][:].bitcast(I32).rearrange("p (c i t) -> p c t i", t=PACK, i=LINE),
+                )
+            nc.vector.tensor_copy(
+                out=wd_plane[:].rearrange("p (t c i) -> p c t i", t=PACK, i=16),
+                in_=w_plane[:].rearrange("p (c i t) -> p c t i", t=PACK, i=16),
+            )
+
+        rounded = [[tile("rounded%d%d" % (a, d), [P, 2, HALF, 2], BF16) for d in range(3)] for a in range(2)]
+        pair = [{d: tile("pair%d%d" % (a, d), [P, 2, HALF, 2], BF16) for d in ops} for a in range(2)]
+        back = {}
+
+        def fetch(a, u, tags):
+            if True:
+                if u == 0:
+                    back[a] = bank(6 + a, "back%d" % a)
+                sums = bank(4 + u, "sums%d%d" % (a, u))
+                g = [tile("g%d%d%d" % (a, d, u), [P, 2, HALF], F32, tags[d]) for d in range(3)]
+                for e in range(2):
+                    for d in range(3):
+                        offsets = pos_sb[d][:, HALF // 16 * a : HALF // 16 * (a + 1)]
+                        nc.vector.tensor_copy(out=g[d][:, e, :], in_=h[2 * u + e][:].indirect(offsets))
+                        nc.tensor.matmul(
+                            out=sums[:, P * e : P * (e + 1)],
+                            lhsT=g[d][:, e, :],
+                            rhs=identity[:],
+                            is_transpose=True,
+                            start=(d == 0),
+                            stop=(d == 2),
+                        )
+                        if e == 1:
+                            nc.scalar.copy(
+                                out=rounded[a][d][:, u].rearrange("p (c i) e -> p c e i", i=LINE),
+                                in_=g[d][:].rearrange("p e (c i) -> p c e i", i=LINE),
+                            )
+                turned = tile("turned%d%d" % (a, u), [P, P, 2], BF16)
+                nc.scalar.activation(
+                    out=turned[:],
+                    in_=sums[:, 0 : 2 * P].rearrange("v (e p) -> v p e", e=2),
+                    func=COPY,
+                    scale=1.0 / 3.0,
+                )
+                nc.tensor.transpose(
+                    back[a][:, P * u : P * (u + 1)], turned[:].rearrange("v p e -> v (p e)").bitcast(F32), identity[:]
+                )
+                for d, op in ops.items():
+                    nc.vector.tensor_tensor(out=pair[a][d][:, u], in0=rounded[a][0][:, u], in1=rounded[a][1][:, u], op=op)
+
+        def finish(a):
+            z_bf = [tile("z_bf%d%d" % (a, d), [P, HALF * PACK], BF16) for d in range(3)]
+            nc.scalar.copy(
+                out=z_bf[0][:].bitcast(F32).rearrange("p (v u) -> p v u", u=2),
+                in_=back[a][:, 0 : 2 * P].rearrange("p (u v) -> p v u", u=2),
+            )
+            for d, op in ops.items():
+                nc.vector.tensor_tensor(
+                    out=z_bf[d][:].rearrange("p (v u e) -> p v u e", u=2, e=2),
+                    in0=pair[a][d][:].rearrange("p u v e -> p v u e"),
+                    in1=rounded[a][2][:].rearrange("p u v e -> p v u e"),
+                    op=op,
+                )
+            return z_bf
+
+        def second_product(a, z_bf):
+            acc = [bank(2 * a + u, "y_acc%d%d" % (a, u)) for u in range(2)]
+            for d in order:
+                z_codes = tile("z_codes%d%d" % (a, d), [P, HALF], U32)
+                z_plane = tile("z_plane%d%d" % (a, d), [P, HALF], U8)
+                nc.vector.quantize_mx(out=z_codes[:].bitcast(FP8X4), scales=z_plane[:], in_=z_bf[d][:])
+                for t in range(PACK):
+                    cols = slice(P * t, P * (t + 1))
+                    nc.tensor.matmul_mx(
+                        out=acc[t // 2][:, HALF * (t % 2) : HALF * (t % 2 + 1)],
+                        lhsT=wd_codes[d][:, cols].bitcast(FP8X4),
+                        lhsT_scale=wd_plane[4 * d : P, cols],
+                        rhs=z_codes[:].bitcast(FP8X4),
+                        rhs_scale=z_plane[:],
+                        start=(d == order[0] and t % 2 == 0),
+                        stop=(d == order[-1] and t % 2 == 1),
+                    )
+            return acc
+
+        def store_values(a, acc, second_copy):
+            y = tile("y%d" % a, [P, PACK, HALF], F32)
+            y_flat = y[:].rearrange("p t v -> p (t v)")
+            nc.scalar.copy(out=y_flat[:, 0 : 2 * HALF], in_=acc[0][:, 0 : 2 * HALF])
+            second_copy(out=y_flat[:, 2 * HALF : 4 * HALF], in_=acc[1][:, 0 : 2 * HALF])
+            nc.sync.dma_start(out=out_rows[:, :, HALF * a : HALF * (a + 1)], in_=y[:])
+            return y
+
+        def store_codes(a, y, tag):
+            cols = slice(HALF * a, HALF * (a + 1))
+            y_bf = tile("y_bf%d" % a, [P, HALF, PACK], BF16, tag)
+            nc.vector.tensor_copy(
+                out=y_bf[:].rearrange("p (c i) t -> p c t i", i=LINE),
+                in_=y[:].rearrange("p t (c i) -> p c t i", i=LINE),
+            )
+            nc.vector.quantize_mx(
+                out=y_codes[:, cols].bitcast(FP8X4),
+                scales=y_plane[:, cols],
+                in_=y_bf[:].rearrange("p v t -> p (v t)"),
+            )
+            nc.sync.dma_start(out=out_words[:, cols], in_=y_codes[:, cols].bitcast(I32))
+
+        fetch(0, 0, ["ring0", "ring1", "ring2"])
+        fetch(0, 1, ["", "", ""])
+        z_first = finish(0)
+        deal()
+        acc_first = second_product(0, z_first)
+        fetch(1, 0, ["ring0", "ring1", "ring2"])
+        y_first = store_values(0, acc_first, nc.scalar.copy)
+        fetch(1, 1, ["z_codes01", "z_codes02", "z_codes00"])
+        acc_second = second_product(1, finish(1))
+        store_codes(0, y_first, "z_bf10")
+        y_second = store_values(1, acc_second, nc.vector.tensor_copy)
+        store_codes(1, y_second, "")
+        for q in range(4):
+            queue = nc.scalar if q % 2 else nc.sync
+            queue.dma_start(
+                out=out_2[0, 4 * q : 4 * q + 4, :].bitcast(I32),
+                in_=y_plane[32 * q : 32 * q + 4, :].bitcast(I32),
+            )

@@ -21,7 +21,7 @@ PACK = 4
 HALF = V // 2
 LINE = 4
 M_HALF = P // 2
-M_VECTOR = 40
+M_VECTOR = 32
 
 
 def as_words(words):
@@ -59,7 +59,7 @@ def tile_picked_pna_none_po_kernel(
         identity = tile("identity", [P, P], F32)
 
         nc.vector.memset(x_plane[:].bitcast(I32), 0)
-        nc.vector.memset(w_plane[:].bitcast(I32), 0)
+        nc.gpsimd.memset(w_plane[:].bitcast(I32), 0)
         make_identity(nc, identity[:])
 
         w1_rows = w1.rearrange("(p j) c -> p j c", j=PACK)
@@ -147,47 +147,55 @@ def tile_picked_pna_none_po_kernel(
                 in_=w_plane[:].rearrange("p (c i t) -> p c t i", t=PACK, i=16),
             )
 
-        rounded = [[tile("rounded%d%d" % (a, d), [P, 2, HALF, 2], BF16) for d in range(3)] for a in range(2)]
-        pair = [{d: tile("pair%d%d" % (a, d), [P, 2, HALF, 2], BF16) for d in ops} for a in range(2)]
-        back = {}
+        rounded = [[tile("rounded%d%d" % (d, u), [P, V, 2], BF16) for u in range(2)] for d in range(2)]
+        rounded_last = tile("rounded_last", [P, 2, V, 2], BF16)
+        pair = {d: tile("pair%d" % d, [P, 2, V, 2], BF16) for d in ops}
+        back = [bank(6 + a, "back%d" % a) for a in range(2)]
 
-        def fetch(a, u, tags):
-            if True:
-                if u == 0:
-                    back[a] = bank(6 + a, "back%d" % a)
-                sums = bank(4 + u, "sums%d%d" % (a, u))
-                g = [tile("g%d%d%d" % (a, d, u), [P, 2, HALF], F32, tags[d]) for d in range(3)]
-                for e in range(2):
-                    for d in range(3):
-                        offsets = pos_sb[d][:, HALF // 16 * a : HALF // 16 * (a + 1)]
-                        nc.vector.tensor_copy(out=g[d][:, e, :], in_=h[2 * u + e][:].indirect(offsets))
-                        nc.tensor.matmul(
-                            out=sums[:, P * e : P * (e + 1)],
-                            lhsT=g[d][:, e, :],
-                            rhs=identity[:],
-                            is_transpose=True,
-                            start=(d == 0),
-                            stop=(d == 2),
-                        )
-                        if e == 1:
-                            nc.scalar.copy(
-                                out=rounded[a][d][:, u].rearrange("p (c i) e -> p c e i", i=LINE),
-                                in_=g[d][:].rearrange("p e (c i) -> p c e i", i=LINE),
-                            )
-                turned = tile("turned%d%d" % (a, u), [P, P, 2], BF16)
-                nc.scalar.activation(
-                    out=turned[:],
-                    in_=sums[:, 0 : 2 * P].rearrange("v (e p) -> v p e", e=2),
-                    func=COPY,
-                    scale=1.0 / 3.0,
-                )
-                nc.tensor.transpose(
-                    back[a][:, P * u : P * (u + 1)], turned[:].rearrange("v p e -> v (p e)").bitcast(F32), identity[:]
-                )
-                for d, op in ops.items():
-                    nc.vector.tensor_tensor(out=pair[a][d][:, u], in0=rounded[a][0][:, u], in1=rounded[a][1][:, u], op=op)
+        def round_pairs(d, u, g, first, count):
+            targets = slice(first, first + count)
+            nc.scalar.copy(
+                out=(rounded[d][u][:] if d < 2 else rounded_last[:, u])[:, targets, :].rearrange("p (c i) e -> p c e i", i=LINE),
+                in_=g[:, :, targets].rearrange("p e (c i) -> p c e i", i=LINE),
+            )
+
+        def mean_turned(u, sums, a):
+            turned = tile("turned%d%d" % (a, u), [P, P, 2], BF16)
+            nc.scalar.activation(
+                out=turned[:],
+                in_=sums[:, 2 * P * a : 2 * P * (a + 1)].rearrange("v (e p) -> v p e", e=2),
+                func=COPY,
+                scale=1.0 / 3.0,
+            )
+            nc.tensor.transpose(
+                back[a][:, P * u : P * (u + 1)], turned[:].rearrange("v p e -> v (p e)").bitcast(F32), identity[:]
+            )
+
+        def fetch(u, steps, tags):
+            sums = bank(4 + u, "sums%d" % u)
+            g = [tile("g%d%d" % (d, u), [P, 2, V], F32, tags[d]) for d in range(3)]
+            for e, d in steps:
+                nc.vector.tensor_copy(out=g[d][:, e, :], in_=h[2 * u + e][:].indirect(pos_sb[d][:]))
+                for a in range(2):
+                    nc.tensor.matmul(
+                        out=sums[:, P * (2 * a + e) : P * (2 * a + e + 1)],
+                        lhsT=g[d][:, e, HALF * a : HALF * (a + 1)],
+                        rhs=identity[:],
+                        is_transpose=True,
+                        start=((e, d) == steps[0] and a == 0),
+                        stop=((e, d) == steps[-1] and a == 1),
+                    )
+                if e == 1 and (u, d) != (1, 2):
+                    round_pairs(d, u, g[d], 0, V)
+            for a in range(2):
+                if u == 1:
+                    round_pairs(2, u, g[2], HALF * a, HALF)
+                mean_turned(u, sums, a)
+            for d, op in ops.items():
+                nc.vector.tensor_tensor(out=pair[d][:, u], in0=rounded[0][u][:], in1=rounded[1][u][:], op=op)
 
         def finish(a):
+            targets = slice(HALF * a, HALF * (a + 1))
             z_bf = [tile("z_bf%d%d" % (a, d), [P, HALF * PACK], BF16) for d in range(3)]
             nc.scalar.copy(
                 out=z_bf[0][:].bitcast(F32).rearrange("p (v u) -> p v u", u=2),
@@ -196,8 +204,8 @@ def tile_picked_pna_none_po_kernel(
             for d, op in ops.items():
                 nc.vector.tensor_tensor(
                     out=z_bf[d][:].rearrange("p (v u e) -> p v u e", u=2, e=2),
-                    in0=pair[a][d][:].rearrange("p u v e -> p v u e"),
-                    in1=rounded[a][2][:].rearrange("p u v e -> p v u e"),
+                    in0=pair[d][:, :, targets, :].rearrange("p u v e -> p v u e"),
+                    in1=rounded_last[:, :, targets, :].rearrange("p u v e -> p v u e"),
                     op=op,
                 )
             return z_bf
@@ -243,15 +251,12 @@ def tile_picked_pna_none_po_kernel(
             )
             nc.sync.dma_start(out=out_words[:, cols], in_=y_codes[:, cols].bitcast(I32))
 
-        fetch(0, 0, ["ring0", "ring1", "ring2"])
-        fetch(0, 1, ["", "", ""])
-        z_first = finish(0)
+        fetch(0, [(e, d) for e in range(2) for d in range(3)], ["", "", ""])
         deal()
-        acc_first = second_product(0, z_first)
-        fetch(1, 0, ["ring0", "ring1", "ring2"])
-        y_first = store_values(0, acc_first, nc.scalar.copy)
-        fetch(1, 1, ["z_codes01", "z_codes02", "z_codes00"])
+        fetch(1, [(e, d) for d in range(3) for e in range(2)], ["w_codes2", "rounded00", "w_plane"])
+        acc_first = second_product(0, finish(0))
         acc_second = second_product(1, finish(1))
+        y_first = store_values(0, acc_first, nc.scalar.copy)
         store_codes(0, y_first, "z_bf10")
         y_second = store_values(1, acc_second, nc.vector.tensor_copy)
         store_codes(1, y_second, "")

@@ -127,7 +127,7 @@ def tile_picked_pna_none_po_kernel(
         for t in range(1, PACK):
             first_product(t, t, 0, S, nc.scalar.copy)
 
-        wd_codes = [tile("wd_codes%d" % d, [P, H], U32) for d in range(3)]
+        wd_codes = [tile("wd_codes%d" % d, [P, H], U32, tag) for d, tag in enumerate(("w1_bf", "w1_codes", "w1_plane"))]
         wd_plane = tile("wd_plane", [P, H], U8)
         y_codes = tile("y_codes", [P, V], U32)
         y_plane = tile("y_plane", [P, V], U8)
@@ -138,13 +138,13 @@ def tile_picked_pna_none_po_kernel(
 
         def deal():
             for d in range(3):
-                nc.vector.tensor_copy(
-                    out=wd_codes[d][:].bitcast(I32).rearrange("p (t c i) -> p c t i", t=PACK, i=LINE),
-                    in_=w_codes[d][:].bitcast(I32).rearrange("p (c i t) -> p c t i", t=PACK, i=LINE),
+                nc.gpsimd.tensor_copy(
+                    out=wd_codes[d][:].bitcast(I32).rearrange("p (t m) -> p t m", t=PACK),
+                    in_=w_codes[d][:].bitcast(I32).rearrange("p (m t) -> p t m", t=PACK),
                 )
-            nc.vector.tensor_copy(
-                out=wd_plane[:].rearrange("p (t c i) -> p c t i", t=PACK, i=16),
-                in_=w_plane[:].rearrange("p (c i t) -> p c t i", t=PACK, i=16),
+            nc.gpsimd.tensor_copy(
+                out=wd_plane[:].rearrange("p (t m) -> p t m", t=PACK),
+                in_=w_plane[:].rearrange("p (m t) -> p t m", t=PACK),
             )
 
         rounded = [[tile("rounded%d%d" % (d, u), [P, V, 2], BF16) for u in range(2)] for d in range(2)]
@@ -210,30 +210,33 @@ def tile_picked_pna_none_po_kernel(
                 )
             return z_bf
 
-        def second_product(a, z_bf):
-            acc = [bank(2 * a + u, "y_acc%d%d" % (a, u)) for u in range(2)]
+        def second_product(a, z_bf, banks):
+            acc = [bank(number, "y_acc%d%d" % (a, number)) for number in banks]
+            per_bank = PACK // len(banks)
             for d in order:
                 z_codes = tile("z_codes%d%d" % (a, d), [P, HALF], U32)
                 z_plane = tile("z_plane%d%d" % (a, d), [P, HALF], U8)
                 nc.vector.quantize_mx(out=z_codes[:].bitcast(FP8X4), scales=z_plane[:], in_=z_bf[d][:])
                 for t in range(PACK):
                     cols = slice(P * t, P * (t + 1))
+                    place = t % per_bank
                     nc.tensor.matmul_mx(
-                        out=acc[t // 2][:, HALF * (t % 2) : HALF * (t % 2 + 1)],
+                        out=acc[t // per_bank][:, HALF * place : HALF * (place + 1)],
                         lhsT=wd_codes[d][:, cols].bitcast(FP8X4),
                         lhsT_scale=wd_plane[4 * d : P, cols],
                         rhs=z_codes[:].bitcast(FP8X4),
                         rhs_scale=z_plane[:],
-                        start=(d == order[0] and t % 2 == 0),
-                        stop=(d == order[-1] and t % 2 == 1),
+                        start=(d == order[0] and place == 0),
+                        stop=(d == order[-1] and place == per_bank - 1),
                     )
             return acc
 
-        def store_values(a, acc, second_copy):
+        def store_values(a, acc, copies):
             y = tile("y%d" % a, [P, PACK, HALF], F32)
             y_flat = y[:].rearrange("p t v -> p (t v)")
-            nc.scalar.copy(out=y_flat[:, 0 : 2 * HALF], in_=acc[0][:, 0 : 2 * HALF])
-            second_copy(out=y_flat[:, 2 * HALF : 4 * HALF], in_=acc[1][:, 0 : 2 * HALF])
+            width = PACK * HALF // len(acc)
+            for n, copy in enumerate(copies):
+                copy(out=y_flat[:, width * n : width * (n + 1)], in_=acc[n][:, 0:width])
             nc.sync.dma_start(out=out_rows[:, :, HALF * a : HALF * (a + 1)], in_=y[:])
             return y
 
@@ -253,12 +256,12 @@ def tile_picked_pna_none_po_kernel(
 
         fetch(0, [(e, d) for e in range(2) for d in range(3)], ["", "", ""])
         deal()
-        fetch(1, [(e, d) for d in range(3) for e in range(2)], ["w_codes2", "rounded00", "w_plane"])
-        acc_first = second_product(0, finish(0))
-        acc_second = second_product(1, finish(1))
-        y_first = store_values(0, acc_first, nc.scalar.copy)
+        fetch(1, [(e, d) for d in range(3) for e in range(2)], ["", "rounded00", ""])
+        acc_first = second_product(0, finish(0), (0, 1))
+        acc_second = second_product(1, finish(1), (2, 3, 4, 5))
+        y_first = store_values(0, acc_first, [nc.scalar.copy] * 2)
         store_codes(0, y_first, "z_bf10")
-        y_second = store_values(1, acc_second, nc.vector.tensor_copy)
+        y_second = store_values(1, acc_second, [nc.scalar.copy, nc.vector.tensor_copy] * 2)
         store_codes(1, y_second, "")
         for q in range(4):
             queue = nc.scalar if q % 2 else nc.sync

@@ -21,7 +21,7 @@ PACK = 4
 HALF = V // 2
 LINE = 4
 M_HALF = P // 2
-M_VECTOR = 32
+M_VECTOR = 40
 
 
 def as_words(words):
@@ -134,7 +134,6 @@ def tile_picked_pna_none_po_kernel(
         out_rows = out_0.rearrange("(p t) v -> p t v", t=PACK)
         out_words = as_words(out_1)
         ops = {1: ALU.max, 2: ALU.min}
-        order = (1, 2, 0)
 
         def deal():
             for d in range(3):
@@ -147,23 +146,15 @@ def tile_picked_pna_none_po_kernel(
                 in_=w_plane[:].rearrange("p (m t) -> p t m", t=PACK),
             )
 
-        rounded = [[tile("rounded%d%d" % (d, u), [P, V, 2], BF16) for u in range(2)] for d in range(2)]
-        rounded_last = tile("rounded_last", [P, 2, V, 2], BF16)
-        pair = {d: tile("pair%d" % d, [P, 2, V, 2], BF16) for d in ops}
+        rounded = [tile("rounded%d" % d, [P, 2, V, 2], BF16) for d in range(3)]
+        pair = [{d: tile("pair%d%d" % (a, d), [P, 2, HALF, 2], BF16) for d in ops} for a in range(2)]
         back = [bank(6 + a, "back%d" % a) for a in range(2)]
 
-        def round_pairs(d, u, g, first, count):
-            targets = slice(first, first + count)
-            nc.scalar.copy(
-                out=(rounded[d][u][:] if d < 2 else rounded_last[:, u])[:, targets, :].rearrange("p (c i) e -> p c e i", i=LINE),
-                in_=g[:, :, targets].rearrange("p e (c i) -> p c e i", i=LINE),
-            )
-
-        def mean_turned(u, sums, a):
+        def mean_turned(u, a, sums):
             turned = tile("turned%d%d" % (a, u), [P, P, 2], BF16)
             nc.scalar.activation(
                 out=turned[:],
-                in_=sums[:, 2 * P * a : 2 * P * (a + 1)].rearrange("v (e p) -> v p e", e=2),
+                in_=sums.rearrange("v (e p) -> v p e", e=2),
                 func=COPY,
                 scale=1.0 / 3.0,
             )
@@ -171,65 +162,94 @@ def tile_picked_pna_none_po_kernel(
                 back[a][:, P * u : P * (u + 1)], turned[:].rearrange("v p e -> v (p e)").bitcast(F32), identity[:]
             )
 
-        def fetch(u, steps, tags):
-            sums = bank(4 + u, "sums%d" % u)
-            g = [tile("g%d%d" % (d, u), [P, 2, V], F32, tags[d]) for d in range(3)]
-            for e, d in steps:
-                nc.vector.tensor_copy(out=g[d][:, e, :], in_=h[2 * u + e][:].indirect(pos_sb[d][:]))
-                for a in range(2):
-                    nc.tensor.matmul(
-                        out=sums[:, P * (2 * a + e) : P * (2 * a + e + 1)],
-                        lhsT=g[d][:, e, HALF * a : HALF * (a + 1)],
-                        rhs=identity[:],
-                        is_transpose=True,
-                        start=((e, d) == steps[0] and a == 0),
-                        stop=((e, d) == steps[-1] and a == 1),
-                    )
-                if e == 1 and (u, d) != (1, 2):
-                    round_pairs(d, u, g[d], 0, V)
-            for a in range(2):
-                if u == 1:
-                    round_pairs(2, u, g[2], HALF * a, HALF)
-                mean_turned(u, sums, a)
-            for d, op in ops.items():
-                nc.vector.tensor_tensor(out=pair[d][:, u], in0=rounded[0][u][:], in1=rounded[1][u][:], op=op)
+        def add_turned(sums, e, values, start, stop):
+            nc.tensor.matmul(
+                out=sums[:, P * e : P * (e + 1)], lhsT=values, rhs=identity[:], is_transpose=True, start=start, stop=stop
+            )
 
-        def finish(a):
+        def pair_up(a, d):
             targets = slice(HALF * a, HALF * (a + 1))
-            z_bf = [tile("z_bf%d%d" % (a, d), [P, HALF * PACK], BF16) for d in range(3)]
+            nc.vector.tensor_tensor(
+                out=pair[a][d][:], in0=rounded[0][:, :, targets, :], in1=rounded[1][:, :, targets, :], op=ops[d]
+            )
+
+        def round_pairs(d, u, g, first):
             nc.scalar.copy(
-                out=z_bf[0][:].bitcast(F32).rearrange("p (v u) -> p v u", u=2),
+                out=rounded[d][:, u, first : first + g.shape[2], :].rearrange("p (c i) e -> p c e i", i=LINE),
+                in_=g.rearrange("p e (c i) -> p c e i", i=LINE),
+            )
+
+        def fetch_first_pair():
+            both = bank(4, "sums0")
+            sums = [both[:, 2 * P * a : 2 * P * (a + 1)] for a in range(2)]
+            g = [tile("g%d0" % d, [P, 2, V], F32) for d in range(3)]
+            for e in range(2):
+                for d in range(3):
+                    nc.vector.tensor_copy(out=g[d][:, e, :], in_=h[e][:].indirect(pos_sb[d][:]))
+                    for a in range(2):
+                        add_turned(
+                            sums[a], e, g[d][:, e, HALF * a : HALF * (a + 1)],
+                            (e, d, a) == (0, 0, 0), (e, d, a) == (1, 2, 1),
+                        )
+                    if e == 1:
+                        round_pairs(d, 0, g[d][:], 0)
+            for a in range(2):
+                mean_turned(0, a, sums[a])
+
+        def fetch_second_pair():
+            held = [bank(number, "sums1%d" % a) for a, number in enumerate((5, 3))]
+            sums = [held[a][:, 0 : 2 * P] for a in range(2)]
+            for d in range(2):
+                g = tile("g%d1" % d, [P, 2, V], F32)
+                for e in range(2):
+                    nc.vector.tensor_copy(out=g[:, e, :], in_=h[2 + e][:].indirect(pos_sb[d][:]))
+                    for a in range(2):
+                        add_turned(sums[a], e, g[:, e, HALF * a : HALF * (a + 1)], (d, e) == (0, 0), False)
+                round_pairs(d, 1, g[:], 0)
+            return sums
+
+        def fetch_last(a, sums):
+            g = tile("g21%d" % a, [P, 2, HALF], F32)
+            columns = slice(HALF // 16 * a, HALF // 16 * (a + 1))
+            for e in range(2):
+                nc.vector.tensor_copy(out=g[:, e, :], in_=h[2 + e][:].indirect(pos_sb[2][:, columns]))
+                add_turned(sums, e, g[:, e, :], False, e == 1)
+            return g
+
+        z_bf = [[tile("z_bf%d%d" % (a, d), [P, HALF * PACK], BF16) for d in range(3)] for a in range(2)]
+
+        def mean_back(a):
+            nc.scalar.copy(
+                out=z_bf[a][0][:].bitcast(F32).rearrange("p (v u) -> p v u", u=2),
                 in_=back[a][:, 0 : 2 * P].rearrange("p (u v) -> p v u", u=2),
             )
-            for d, op in ops.items():
-                nc.vector.tensor_tensor(
-                    out=z_bf[d][:].rearrange("p (v u e) -> p v u e", u=2, e=2),
-                    in0=pair[d][:, :, targets, :].rearrange("p u v e -> p v u e"),
-                    in1=rounded_last[:, :, targets, :].rearrange("p u v e -> p v u e"),
-                    op=op,
-                )
-            return z_bf
 
-        def second_product(a, z_bf, banks):
-            acc = [bank(number, "y_acc%d%d" % (a, number)) for number in banks]
-            per_bank = PACK // len(banks)
-            for d in order:
-                z_codes = tile("z_codes%d%d" % (a, d), [P, HALF], U32)
-                z_plane = tile("z_plane%d%d" % (a, d), [P, HALF], U8)
-                nc.vector.quantize_mx(out=z_codes[:].bitcast(FP8X4), scales=z_plane[:], in_=z_bf[d][:])
-                for t in range(PACK):
-                    cols = slice(P * t, P * (t + 1))
-                    place = t % per_bank
-                    nc.tensor.matmul_mx(
-                        out=acc[t // per_bank][:, HALF * place : HALF * (place + 1)],
-                        lhsT=wd_codes[d][:, cols].bitcast(FP8X4),
-                        lhsT_scale=wd_plane[4 * d : P, cols],
-                        rhs=z_codes[:].bitcast(FP8X4),
-                        rhs_scale=z_plane[:],
-                        start=(d == order[0] and place == 0),
-                        stop=(d == order[-1] and place == per_bank - 1),
-                    )
-            return acc
+        def extreme(a, d):
+            targets = slice(HALF * a, HALF * (a + 1))
+            nc.vector.tensor_tensor(
+                out=z_bf[a][d][:].rearrange("p (v u e) -> p v u e", u=2, e=2),
+                in0=pair[a][d][:].rearrange("p u v e -> p v u e"),
+                in1=rounded[2][:, :, targets, :].rearrange("p u v e -> p v u e"),
+                op=ops[d],
+            )
+
+        def second_product(a, d, acc, order):
+            per_bank = PACK // len(acc)
+            z_codes = tile("z_codes%d%d" % (a, d), [P, HALF], U32)
+            z_plane = tile("z_plane%d%d" % (a, d), [P, HALF], U8)
+            nc.vector.quantize_mx(out=z_codes[:].bitcast(FP8X4), scales=z_plane[:], in_=z_bf[a][d][:])
+            for t in range(PACK):
+                cols = slice(P * t, P * (t + 1))
+                place = t % per_bank
+                nc.tensor.matmul_mx(
+                    out=acc[t // per_bank][:, HALF * place : HALF * (place + 1)],
+                    lhsT=wd_codes[d][:, cols].bitcast(FP8X4),
+                    lhsT_scale=wd_plane[4 * d : P, cols],
+                    rhs=z_codes[:].bitcast(FP8X4),
+                    rhs_scale=z_plane[:],
+                    start=(d == order[0] and place == 0),
+                    stop=(d == order[-1] and place == per_bank - 1),
+                )
 
         def store_values(a, acc, copies):
             y = tile("y%d" % a, [P, PACK, HALF], F32)
@@ -254,13 +274,36 @@ def tile_picked_pna_none_po_kernel(
             )
             nc.sync.dma_start(out=out_words[:, cols], in_=y_codes[:, cols].bitcast(I32))
 
-        fetch(0, [(e, d) for e in range(2) for d in range(3)], ["", "", ""])
+        fetch_first_pair()
         deal()
-        fetch(1, [(e, d) for d in range(3) for e in range(2)], ["", "rounded00", ""])
-        acc_first = second_product(0, finish(0), (0, 1))
-        acc_second = second_product(1, finish(1), (2, 3, 4, 5))
+        sums = fetch_second_pair()
+        g_first = fetch_last(0, sums[0])
+        g_second = fetch_last(1, sums[1])
+        round_pairs(2, 1, g_first[:], 0)
+        mean_turned(1, 0, sums[0])
+        round_pairs(2, 1, g_second[:], HALF)
+        mean_back(0)
+        mean_turned(1, 1, sums[1])
+        mean_back(1)
+        acc_first = [bank(number, "y_acc0%d" % number) for number in (0, 1)]
+        acc_second = [bank(number, "y_acc1%d" % number) for number in (2, 4, 5, 3)]
+        order_first, order_second = (1, 2, 0), (1, 0, 2)
+        pair_up(0, 1)
+        pair_up(0, 2)
+        extreme(0, 1)
+        extreme(0, 2)
+        second_product(0, 1, acc_first, order_first)
+        second_product(0, 2, acc_first, order_first)
+        pair_up(1, 1)
+        second_product(0, 0, acc_first, order_first)
+        extreme(1, 1)
+        pair_up(1, 2)
+        second_product(1, 1, acc_second, order_second)
+        extreme(1, 2)
+        second_product(1, 0, acc_second, order_second)
+        second_product(1, 2, acc_second, order_second)
         y_first = store_values(0, acc_first, [nc.scalar.copy] * 2)
-        store_codes(0, y_first, "z_bf10")
+        store_codes(0, y_first, "z_bf12")
         y_second = store_values(1, acc_second, [nc.scalar.copy, nc.vector.tensor_copy] * 2)
         store_codes(1, y_second, "")
         for q in range(4):

@@ -18,20 +18,27 @@ COPY = mybir.ActivationFunctionType.Copy
 
 P = 128
 PACK = 4
+LISTS = 3
 HALF = V // 2
 LINE = 4
-M_HALF = P // 2
-M_VECTOR = 40
+GROUPS = P // 2
+GROUPS_VECTOR = 52
+MEAN, LARGEST, SMALLEST = 0, 1, 2
+EXTREME_OP = {LARGEST: ALU.max, SMALLEST: ALU.min}
 
 
 def as_words(words):
     return words[0].rearrange("p n r -> p (n r)").bitcast(I32)
 
 
-def load_scale_rows(queue, plane, first_row, scales, quadrants=range(4)):
-    for q in quadrants:
+def load_scale_rows(nc, plane, first_row, scales):
+    for q in range(4):
         row = 32 * q + first_row
-        queue.dma_start(out=plane[row : row + 4, :].bitcast(I32), in_=scales[0, 4 * q : 4 * q + 4, :].bitcast(I32))
+        nc.sync.dma_start(out=plane[row : row + 4, :].bitcast(I32), in_=scales[0, 4 * q : 4 * q + 4, :].bitcast(I32))
+
+
+def half_of_targets(a):
+    return slice(HALF * a, HALF * (a + 1))
 
 
 def tile_picked_pna_none_po_kernel(
@@ -43,18 +50,18 @@ def tile_picked_pna_none_po_kernel(
         sb = ctx.enter_context(tc.tile_pool(name="sb", bufs=1))
         ps = ctx.enter_context(tc.psum_pool(name="ps", bufs=1))
 
-        def tile(name, shape, dtype, tag=""):
-            return sb.tile(shape, dtype, name=name, tag=tag or name, align_bytes=64)
+        def tile(name, shape, dtype, after=""):
+            return sb.tile(shape, dtype, name=name, tag=after or name, align_bytes=64)
 
         def bank(number, name):
             return ps.tile([P, 512], F32, name=name, tag="bank%d" % number)
 
         offs_sb = tile("offs_sb", [P, S // 16], U16)
-        pos_sb = [tile("pos_sb%d" % d, [P, V // 16], U16) for d in range(3)]
+        pos_sb = [tile("pos_sb%d" % d, [P, V // 16], U16) for d in range(LISTS)]
         x_plane = tile("x_plane", [P, T], U8)
         x_codes = tile("x_codes", [P, T], U32)
-        w1_raw = [tile("w1_raw%d" % a, [P, PACK, H // 2], F32) for a in range(2)]
-        w_codes = [tile("w_codes%d" % d, [P, H], U32) for d in range(3)]
+        w1_raw = [tile("w1_raw%d" % b, [P, PACK, H // 2], F32) for b in range(2)]
+        w_codes = [tile("w_codes%d" % kind, [P, H], U32) for kind in range(3)]
         w_plane = tile("w_plane", [P, H], U8)
         identity = tile("identity", [P, P], F32)
 
@@ -63,19 +70,18 @@ def tile_picked_pna_none_po_kernel(
         make_identity(nc, identity[:])
 
         w1_rows = w1.rearrange("(p j) c -> p j c", j=PACK)
-        words_in = (w2_words, w3_words, w4_words)
         nc.sync.dma_start(out=offs_sb[:], in_=offs)
         nc.sync.dma_start(out=x_codes[:].bitcast(I32), in_=as_words(x_words))
         nc.sync.dma_start(out=pos_sb[0][:], in_=pos1)
-        load_scale_rows(nc.sync, x_plane, 0, x_scales)
+        load_scale_rows(nc, x_plane, 0, x_scales)
         nc.sync.dma_start(out=w1_raw[0][:], in_=w1_rows[:, :, 0 : H // 2])
         nc.sync.dma_start(out=w1_raw[1][:], in_=w1_rows[:, :, H // 2 : H])
         nc.sync.dma_start(out=pos_sb[1][:], in_=pos2)
         nc.sync.dma_start(out=pos_sb[2][:], in_=pos3)
-        for d in range(3):
-            nc.sync.dma_start(out=w_codes[d][:].bitcast(I32), in_=as_words(words_in[d]))
-        for d, scales in enumerate((w2_scales, w3_scales, w4_scales)):
-            load_scale_rows(nc.sync, w_plane, 4 * d, scales)
+        for kind, words in enumerate((w2_words, w3_words, w4_words)):
+            nc.sync.dma_start(out=w_codes[kind][:].bitcast(I32), in_=as_words(words))
+        for kind, scales in enumerate((w2_scales, w3_scales, w4_scales)):
+            load_scale_rows(nc, w_plane, 4 * kind, scales)
 
         xp_plane = tile("xp_plane", [P, S], U8)
         xp_codes = tile("xp_codes", [P, S], U32)
@@ -84,16 +90,16 @@ def tile_picked_pna_none_po_kernel(
 
         w1_bf = tile("w1_bf", [P, PACK, P, PACK], BF16)
 
-        def w1_views(a, m0, m1):
-            dst = w1_bf[:, :, M_HALF * a + m0 : M_HALF * a + m1, :].rearrange("p t m j -> p m t j")
-            src = w1_raw[a][:, :, PACK * m0 : PACK * m1].rearrange("p j (m t) -> p m t j", t=PACK)
+        def w1_views(b, m0, m1):
+            dst = w1_bf[:, :, GROUPS * b + m0 : GROUPS * b + m1, :].rearrange("p t m j -> p m t j")
+            src = w1_raw[b][:, :, PACK * m0 : PACK * m1].rearrange("p j (m t) -> p m t j", t=PACK)
             return dst, src
 
-        dst, src = w1_views(0, 0, M_HALF)
+        dst, src = w1_views(0, 0, GROUPS)
         nc.scalar.activation(out=dst, in_=src, func=COPY)
-        dst, src = w1_views(1, 0, M_VECTOR)
+        dst, src = w1_views(1, 0, GROUPS_VECTOR)
         nc.vector.tensor_copy(out=dst, in_=src)
-        dst, src = w1_views(1, M_VECTOR, M_HALF)
+        dst, src = w1_views(1, GROUPS_VECTOR, GROUPS)
         nc.scalar.copy(out=dst, in_=src)
 
         w1_codes = tile("w1_codes", [P, H], U32)
@@ -127,128 +133,131 @@ def tile_picked_pna_none_po_kernel(
         for t in range(1, PACK):
             first_product(t, t, 0, S, nc.scalar.copy)
 
-        wd_codes = [tile("wd_codes%d" % d, [P, H], U32, tag) for d, tag in enumerate(("w1_bf", "w1_codes", "w1_plane"))]
+        wd_codes = [
+            tile("wd_codes%d" % kind, [P, H], U32, after)
+            for kind, after in enumerate(("w1_bf", "w1_codes", "w1_plane"))
+        ]
         wd_plane = tile("wd_plane", [P, H], U8)
         y_codes = tile("y_codes", [P, V], U32)
         y_plane = tile("y_plane", [P, V], U8)
         out_rows = out_0.rearrange("(p t) v -> p t v", t=PACK)
         out_words = as_words(out_1)
-        ops = {1: ALU.max, 2: ALU.min}
 
-        def deal():
-            for d in range(3):
+        def deal_weights():
+            for kind in range(3):
                 nc.gpsimd.tensor_copy(
-                    out=wd_codes[d][:].bitcast(I32).rearrange("p (t m) -> p t m", t=PACK),
-                    in_=w_codes[d][:].bitcast(I32).rearrange("p (m t) -> p t m", t=PACK),
+                    out=wd_codes[kind][:].bitcast(I32).rearrange("p (t m) -> p t m", t=PACK),
+                    in_=w_codes[kind][:].bitcast(I32).rearrange("p (m t) -> p t m", t=PACK),
                 )
             nc.gpsimd.tensor_copy(
                 out=wd_plane[:].rearrange("p (t m) -> p t m", t=PACK),
                 in_=w_plane[:].rearrange("p (m t) -> p t m", t=PACK),
             )
 
-        rounded = [tile("rounded%d" % d, [P, 2, V, 2], BF16) for d in range(3)]
-        pair = [{d: tile("pair%d%d" % (a, d), [P, 2, HALF, 2], BF16) for d in ops} for a in range(2)]
-        back = [bank(6 + a, "back%d" % a) for a in range(2)]
-
-        def mean_turned(u, a, sums):
-            turned = tile("turned%d%d" % (a, u), [P, P, 2], BF16)
-            nc.scalar.activation(
-                out=turned[:],
-                in_=sums.rearrange("v (e p) -> v p e", e=2),
-                func=COPY,
-                scale=1.0 / 3.0,
-            )
-            nc.tensor.transpose(
-                back[a][:, P * u : P * (u + 1)], turned[:].rearrange("v p e -> v (p e)").bitcast(F32), identity[:]
-            )
+        rounded = [tile("rounded%d" % d, [P, 2, V, 2], BF16) for d in range(LISTS)]
+        of_two = [{kind: tile("of_two%d%d" % (a, kind), [P, 2, HALF, 2], BF16) for kind in EXTREME_OP} for a in range(2)]
+        mean_back = [bank(6 + a, "mean_back%d" % a) for a in range(2)]
 
         def add_turned(sums, e, values, start, stop):
             nc.tensor.matmul(
                 out=sums[:, P * e : P * (e + 1)], lhsT=values, rhs=identity[:], is_transpose=True, start=start, stop=stop
             )
 
-        def pair_up(a, d):
-            targets = slice(HALF * a, HALF * (a + 1))
-            nc.vector.tensor_tensor(
-                out=pair[a][d][:], in0=rounded[0][:, :, targets, :], in1=rounded[1][:, :, targets, :], op=ops[d]
+        def round_mean(u, a, sums):
+            turned = tile("turned%d%d" % (a, u), [P, P, 2], BF16)
+            nc.scalar.activation(
+                out=turned[:],
+                in_=sums.rearrange("v (e p) -> v p e", e=2),
+                func=COPY,
+                scale=1.0 / LISTS,
+            )
+            nc.tensor.transpose(
+                mean_back[a][:, P * u : P * (u + 1)], turned[:].rearrange("v p e -> v (p e)").bitcast(F32), identity[:]
             )
 
-        def round_pairs(d, u, g, first):
+        def round_pair(d, u, fetched, first):
             nc.scalar.copy(
-                out=rounded[d][:, u, first : first + g.shape[2], :].rearrange("p (c i) e -> p c e i", i=LINE),
-                in_=g.rearrange("p e (c i) -> p c e i", i=LINE),
+                out=rounded[d][:, u, first : first + fetched.shape[2], :].rearrange("p (c i) e -> p c e i", i=LINE),
+                in_=fetched.rearrange("p e (c i) -> p c e i", i=LINE),
             )
 
         def fetch_first_pair():
             both = bank(4, "sums0")
             sums = [both[:, 2 * P * a : 2 * P * (a + 1)] for a in range(2)]
-            g = [tile("g%d0" % d, [P, 2, V], F32) for d in range(3)]
+            fetched = [tile("fetched%d0" % d, [P, 2, V], F32) for d in range(LISTS)]
             for e in range(2):
-                for d in range(3):
-                    nc.vector.tensor_copy(out=g[d][:, e, :], in_=h[e][:].indirect(pos_sb[d][:]))
+                for d in range(LISTS):
+                    nc.vector.tensor_copy(out=fetched[d][:, e, :], in_=h[e][:].indirect(pos_sb[d][:]))
                     for a in range(2):
                         add_turned(
-                            sums[a], e, g[d][:, e, HALF * a : HALF * (a + 1)],
-                            (e, d, a) == (0, 0, 0), (e, d, a) == (1, 2, 1),
+                            sums[a], e, fetched[d][:, e, half_of_targets(a)],
+                            (e, d, a) == (0, 0, 0), (e, d, a) == (1, LISTS - 1, 1),
                         )
                     if e == 1:
-                        round_pairs(d, 0, g[d][:], 0)
+                        round_pair(d, 0, fetched[d][:], 0)
             for a in range(2):
-                mean_turned(0, a, sums[a])
+                round_mean(0, a, sums[a])
 
         def fetch_second_pair():
             held = [bank(number, "sums1%d" % a) for a, number in enumerate((5, 3))]
             sums = [held[a][:, 0 : 2 * P] for a in range(2)]
-            for d in range(2):
-                g = tile("g%d1" % d, [P, 2, V], F32)
+            fetched = [tile("fetched%d1" % d, [P, 2, V], F32) for d in range(LISTS)]
+            for d in range(LISTS):
                 for e in range(2):
-                    nc.vector.tensor_copy(out=g[:, e, :], in_=h[2 + e][:].indirect(pos_sb[d][:]))
+                    last = (d, e) == (LISTS - 1, 1)
+                    if not last:
+                        nc.vector.tensor_copy(out=fetched[d][:, e, :], in_=h[2 + e][:].indirect(pos_sb[d][:]))
                     for a in range(2):
-                        add_turned(sums[a], e, g[:, e, HALF * a : HALF * (a + 1)], (d, e) == (0, 0), False)
-                round_pairs(d, 1, g[:], 0)
-            return sums
+                        values = fetched[d][:, e, half_of_targets(a)]
+                        if last:
+                            offsets = pos_sb[d][:, HALF // 16 * a : HALF // 16 * (a + 1)]
+                            nc.vector.tensor_copy(out=values, in_=h[2 + e][:].indirect(offsets))
+                        add_turned(sums[a], e, values, (d, e) == (0, 0), last)
+                if d < LISTS - 1:
+                    round_pair(d, 1, fetched[d][:], 0)
+            return sums, fetched[LISTS - 1]
 
-        def fetch_last(a, sums):
-            g = tile("g21%d" % a, [P, 2, HALF], F32)
-            columns = slice(HALF // 16 * a, HALF // 16 * (a + 1))
-            for e in range(2):
-                nc.vector.tensor_copy(out=g[:, e, :], in_=h[2 + e][:].indirect(pos_sb[2][:, columns]))
-                add_turned(sums, e, g[:, e, :], False, e == 1)
-            return g
+        z_bf = [[tile("z_bf%d%d" % (a, kind), [P, HALF * PACK], BF16) for kind in range(3)] for a in range(2)]
 
-        z_bf = [[tile("z_bf%d%d" % (a, d), [P, HALF * PACK], BF16) for d in range(3)] for a in range(2)]
-
-        def mean_back(a):
+        def lay_mean(a):
             nc.scalar.copy(
-                out=z_bf[a][0][:].bitcast(F32).rearrange("p (v u) -> p v u", u=2),
-                in_=back[a][:, 0 : 2 * P].rearrange("p (u v) -> p v u", u=2),
+                out=z_bf[a][MEAN][:].bitcast(F32).rearrange("p (v u) -> p v u", u=2),
+                in_=mean_back[a][:, 0 : 2 * P].rearrange("p (u v) -> p v u", u=2),
             )
 
-        def extreme(a, d):
-            targets = slice(HALF * a, HALF * (a + 1))
+        def extreme_of_two(a, kind):
+            targets = half_of_targets(a)
             nc.vector.tensor_tensor(
-                out=z_bf[a][d][:].rearrange("p (v u e) -> p v u e", u=2, e=2),
-                in0=pair[a][d][:].rearrange("p u v e -> p v u e"),
-                in1=rounded[2][:, :, targets, :].rearrange("p u v e -> p v u e"),
-                op=ops[d],
+                out=of_two[a][kind][:],
+                in0=rounded[0][:, :, targets, :],
+                in1=rounded[1][:, :, targets, :],
+                op=EXTREME_OP[kind],
             )
 
-        def second_product(a, d, acc, order):
+        def extreme_of_three(a, kind):
+            nc.vector.tensor_tensor(
+                out=z_bf[a][kind][:].rearrange("p (v u e) -> p v u e", u=2, e=2),
+                in0=of_two[a][kind][:].rearrange("p u v e -> p v u e"),
+                in1=rounded[2][:, :, half_of_targets(a), :].rearrange("p u v e -> p v u e"),
+                op=EXTREME_OP[kind],
+            )
+
+        def second_product(a, kind, acc, kinds):
             per_bank = PACK // len(acc)
-            z_codes = tile("z_codes%d%d" % (a, d), [P, HALF], U32)
-            z_plane = tile("z_plane%d%d" % (a, d), [P, HALF], U8)
-            nc.vector.quantize_mx(out=z_codes[:].bitcast(FP8X4), scales=z_plane[:], in_=z_bf[a][d][:])
+            z_codes = tile("z_codes%d%d" % (a, kind), [P, HALF], U32)
+            z_plane = tile("z_plane%d%d" % (a, kind), [P, HALF], U8)
+            nc.vector.quantize_mx(out=z_codes[:].bitcast(FP8X4), scales=z_plane[:], in_=z_bf[a][kind][:])
             for t in range(PACK):
                 cols = slice(P * t, P * (t + 1))
                 place = t % per_bank
                 nc.tensor.matmul_mx(
                     out=acc[t // per_bank][:, HALF * place : HALF * (place + 1)],
-                    lhsT=wd_codes[d][:, cols].bitcast(FP8X4),
-                    lhsT_scale=wd_plane[4 * d : P, cols],
+                    lhsT=wd_codes[kind][:, cols].bitcast(FP8X4),
+                    lhsT_scale=wd_plane[4 * kind : P, cols],
                     rhs=z_codes[:].bitcast(FP8X4),
                     rhs_scale=z_plane[:],
-                    start=(d == order[0] and place == 0),
-                    stop=(d == order[-1] and place == per_bank - 1),
+                    start=(kind == kinds[0] and place == 0),
+                    stop=(kind == kinds[-1] and place == per_bank - 1),
                 )
 
         def store_values(a, acc, copies):
@@ -257,53 +266,52 @@ def tile_picked_pna_none_po_kernel(
             width = PACK * HALF // len(acc)
             for n, copy in enumerate(copies):
                 copy(out=y_flat[:, width * n : width * (n + 1)], in_=acc[n][:, 0:width])
-            nc.sync.dma_start(out=out_rows[:, :, HALF * a : HALF * (a + 1)], in_=y[:])
+            nc.sync.dma_start(out=out_rows[:, :, half_of_targets(a)], in_=y[:])
             return y
 
-        def store_codes(a, y, tag):
-            cols = slice(HALF * a, HALF * (a + 1))
-            y_bf = tile("y_bf%d" % a, [P, HALF, PACK], BF16, tag)
+        def store_codes(a, y, after):
+            targets = half_of_targets(a)
+            y_bf = tile("y_bf%d" % a, [P, HALF, PACK], BF16, after)
             nc.vector.tensor_copy(
                 out=y_bf[:].rearrange("p (c i) t -> p c t i", i=LINE),
                 in_=y[:].rearrange("p t (c i) -> p c t i", i=LINE),
             )
             nc.vector.quantize_mx(
-                out=y_codes[:, cols].bitcast(FP8X4),
-                scales=y_plane[:, cols],
+                out=y_codes[:, targets].bitcast(FP8X4),
+                scales=y_plane[:, targets],
                 in_=y_bf[:].rearrange("p v t -> p (v t)"),
             )
-            nc.sync.dma_start(out=out_words[:, cols], in_=y_codes[:, cols].bitcast(I32))
+            nc.sync.dma_start(out=out_words[:, targets], in_=y_codes[:, targets].bitcast(I32))
 
         fetch_first_pair()
-        deal()
-        sums = fetch_second_pair()
-        g_first = fetch_last(0, sums[0])
-        g_second = fetch_last(1, sums[1])
-        round_pairs(2, 1, g_first[:], 0)
-        mean_turned(1, 0, sums[0])
-        round_pairs(2, 1, g_second[:], HALF)
-        mean_back(0)
-        mean_turned(1, 1, sums[1])
-        mean_back(1)
+        deal_weights()
+        sums, last_fetched = fetch_second_pair()
+        round_pair(LISTS - 1, 1, last_fetched[:, :, half_of_targets(0)], 0)
+        round_mean(1, 0, sums[0])
+        round_mean(1, 1, sums[1])
+        round_pair(LISTS - 1, 1, last_fetched[:, :, half_of_targets(1)], HALF)
+        lay_mean(0)
+        lay_mean(1)
         acc_first = [bank(number, "y_acc0%d" % number) for number in (0, 1)]
         acc_second = [bank(number, "y_acc1%d" % number) for number in (2, 4, 5, 3)]
-        order_first, order_second = (1, 2, 0), (1, 0, 2)
-        pair_up(0, 1)
-        pair_up(0, 2)
-        extreme(0, 1)
-        extreme(0, 2)
-        second_product(0, 1, acc_first, order_first)
-        second_product(0, 2, acc_first, order_first)
-        pair_up(1, 1)
-        second_product(0, 0, acc_first, order_first)
-        extreme(1, 1)
-        pair_up(1, 2)
-        second_product(1, 1, acc_second, order_second)
-        extreme(1, 2)
-        second_product(1, 0, acc_second, order_second)
-        second_product(1, 2, acc_second, order_second)
+        kinds_first, kinds_second = (LARGEST, SMALLEST, MEAN), (MEAN, LARGEST, SMALLEST)
+        extreme_of_two(0, LARGEST)
+        extreme_of_two(0, SMALLEST)
+        extreme_of_three(0, LARGEST)
+        extreme_of_three(0, SMALLEST)
+        second_product(0, LARGEST, acc_first, kinds_first)
+        second_product(0, SMALLEST, acc_first, kinds_first)
+        extreme_of_two(1, LARGEST)
+        extreme_of_two(1, SMALLEST)
+        second_product(0, MEAN, acc_first, kinds_first)
+        extreme_of_three(1, LARGEST)
+        second_product(1, MEAN, acc_second, kinds_second)
+        extreme_of_three(1, SMALLEST)
+        second_product(1, LARGEST, acc_second, kinds_second)
+        second_product(1, SMALLEST, acc_second, kinds_second)
+
         y_first = store_values(0, acc_first, [nc.scalar.copy] * 2)
-        store_codes(0, y_first, "z_bf12")
+        store_codes(0, y_first, "z_bf%d%d" % (1, SMALLEST))
         y_second = store_values(1, acc_second, [nc.scalar.copy, nc.vector.tensor_copy] * 2)
         store_codes(1, y_second, "")
         for q in range(4):

@@ -104,7 +104,9 @@ def tile_picked_pna_none_po_kernel(
 
         w1_codes = tile("w1_codes", [P, H], U32)
         w1_plane = tile("w1_plane", [P, H], U8)
-        h = [tile("h%d" % t, [P, S], F32) for t in range(PACK)]
+        h_first = [tile("h%d" % t, [P, S], F32) for t in range(2)]
+        h_second = tile("h23", [P, 2, S], F32)
+        h = [h_first[0][:], h_first[1][:], h_second[:, 0], h_second[:, 1]]
         for t in range(PACK):
             cols = slice(P * t, P * (t + 1))
             nc.vector.quantize_mx(
@@ -113,12 +115,10 @@ def tile_picked_pna_none_po_kernel(
                 in_=w1_bf[:, t].rearrange("p m j -> p (m j)"),
             )
 
-        def first_product(t, number, first, count, copy):
+        def first_pass(t, out, picked):
             cols = slice(P * t, P * (t + 1))
-            picked = slice(first, first + count)
-            acc = bank(number, "h_acc%d_%d" % (t, first))
             nc.tensor.matmul_mx(
-                out=acc[:, 0:count],
+                out=out,
                 lhsT=w1_codes[:, cols].bitcast(FP8X4),
                 lhsT_scale=w1_plane[:, cols],
                 rhs=xp_codes[:, picked].bitcast(FP8X4),
@@ -126,12 +126,22 @@ def tile_picked_pna_none_po_kernel(
                 start=True,
                 stop=True,
             )
-            copy(out=h[t][:, picked], in_=acc[:, 0:count])
 
-        first_product(0, 0, 0, S // 2, nc.scalar.copy)
-        first_product(0, 7, S // 2, S // 2, nc.vector.tensor_copy)
-        for t in range(1, PACK):
-            first_product(t, t, 0, S, nc.scalar.copy)
+        for part, number in enumerate((0, 7, 6, 5)):
+            picked = slice(P * part, P * (part + 1))
+            acc = bank(number, "h_acc0%d" % part)
+            first_pass(0, acc[:, 0:P], picked)
+            copy = nc.scalar.copy if part % 2 else nc.vector.tensor_copy
+            copy(out=h[0][:, picked], in_=acc[:, 0:P])
+        acc = bank(1, "h_acc1")
+        first_pass(1, acc[:], slice(0, S))
+        nc.scalar.copy(out=h[1], in_=acc[:])
+        for part in range(2):
+            picked = slice(S // 2 * part, S // 2 * (part + 1))
+            acc = bank(2 + part, "h_acc23%d" % part)
+            for e in range(2):
+                first_pass(2 + e, acc[:, S // 2 * e : S // 2 * (e + 1)], picked)
+            nc.scalar.copy(out=h_second[:, :, picked], in_=acc[:].rearrange("p (e n) -> p e n", e=2))
 
         wd_codes = [
             tile("wd_codes%d" % kind, [P, H], U32, after)
@@ -187,7 +197,7 @@ def tile_picked_pna_none_po_kernel(
             fetched = [tile("fetched%d0" % d, [P, 2, V], F32) for d in range(LISTS)]
             for e in range(2):
                 for d in range(LISTS):
-                    nc.vector.tensor_copy(out=fetched[d][:, e, :], in_=h[e][:].indirect(pos_sb[d][:]))
+                    nc.vector.tensor_copy(out=fetched[d][:, e, :], in_=h[e].indirect(pos_sb[d][:]))
                     for a in range(2):
                         add_turned(
                             sums[a], e, fetched[d][:, e, half_of_targets(a)],
@@ -206,12 +216,12 @@ def tile_picked_pna_none_po_kernel(
                 for e in range(2):
                     last = (d, e) == (LISTS - 1, 1)
                     if not last:
-                        nc.vector.tensor_copy(out=fetched[d][:, e, :], in_=h[2 + e][:].indirect(pos_sb[d][:]))
+                        nc.vector.tensor_copy(out=fetched[d][:, e, :], in_=h[2 + e].indirect(pos_sb[d][:]))
                     for a in range(2):
                         values = fetched[d][:, e, half_of_targets(a)]
                         if last:
                             offsets = pos_sb[d][:, HALF // 16 * a : HALF // 16 * (a + 1)]
-                            nc.vector.tensor_copy(out=values, in_=h[2 + e][:].indirect(offsets))
+                            nc.vector.tensor_copy(out=values, in_=h[2 + e].indirect(offsets))
                         add_turned(sums[a], e, values, (d, e) == (0, 0), last)
                 if d < LISTS - 1:
                     round_pair(d, 1, fetched[d][:], 0)

@@ -72,10 +72,10 @@ def tile_picked_pna_none_po_kernel(
         w1_rows = w1.rearrange("(p j) c -> p j c", j=PACK)
         nc.sync.dma_start(out=offs_sb[:], in_=offs)
         nc.sync.dma_start(out=x_codes[:].bitcast(I32), in_=as_words(x_words))
-        nc.sync.dma_start(out=pos_sb[0][:], in_=pos1)
         load_scale_rows(nc, x_plane, 0, x_scales)
         nc.sync.dma_start(out=w1_raw[0][:], in_=w1_rows[:, :, 0 : H // 2])
         nc.sync.dma_start(out=w1_raw[1][:], in_=w1_rows[:, :, H // 2 : H])
+        nc.sync.dma_start(out=pos_sb[0][:], in_=pos1)
         nc.sync.dma_start(out=pos_sb[1][:], in_=pos2)
         nc.sync.dma_start(out=pos_sb[2][:], in_=pos3)
         for kind, words in enumerate((w2_words, w3_words, w4_words)):
@@ -322,7 +322,7 @@ def tile_picked_pna_none_po_kernel(
 
         y_first = store_values(0, acc_first, [nc.scalar.copy] * 2)
         store_codes(0, y_first, "z_bf%d%d" % (1, SMALLEST))
-        y_second = store_values(1, acc_second, [nc.scalar.copy, nc.vector.tensor_copy] * 2)
+        y_second = store_values(1, acc_second, [nc.vector.tensor_copy, nc.scalar.copy] * 2)
         store_codes(1, y_second, "")
         for q in range(4):
             queue = nc.scalar if q % 2 else nc.sync

@@ -22,7 +22,7 @@ LISTS = 3
 HALF = V // 2
 LINE = 4
 GROUPS = P // 2
-GROUPS_VECTOR = 52
+PARTS = ((0, 256), (256, 128), (384, 128))
 MEAN, LARGEST, SMALLEST = 0, 1, 2
 EXTREME_OP = {LARGEST: ALU.max, SMALLEST: ALU.min}
 
@@ -71,81 +71,88 @@ def tile_picked_pna_none_po_kernel(
 
         w1_rows = w1.rearrange("(p j) c -> p j c", j=PACK)
         nc.sync.dma_start(out=offs_sb[:], in_=offs)
-        nc.sync.dma_start(out=x_codes[:].bitcast(I32), in_=as_words(x_words))
-        load_scale_rows(nc, x_plane, 0, x_scales)
         nc.sync.dma_start(out=w1_raw[0][:], in_=w1_rows[:, :, 0 : H // 2])
+        load_scale_rows(nc, x_plane, 0, x_scales)
         nc.sync.dma_start(out=w1_raw[1][:], in_=w1_rows[:, :, H // 2 : H])
-        nc.sync.dma_start(out=pos_sb[0][:], in_=pos1)
-        nc.sync.dma_start(out=pos_sb[1][:], in_=pos2)
-        nc.sync.dma_start(out=pos_sb[2][:], in_=pos3)
+        nc.sync.dma_start(out=x_codes[:].bitcast(I32), in_=as_words(x_words))
+        for d, pos in enumerate((pos1, pos2, pos3)):
+            nc.sync.dma_start(out=pos_sb[d][:], in_=pos)
         for kind, words in enumerate((w2_words, w3_words, w4_words)):
             nc.sync.dma_start(out=w_codes[kind][:].bitcast(I32), in_=as_words(words))
         for kind, scales in enumerate((w2_scales, w3_scales, w4_scales)):
             load_scale_rows(nc, w_plane, 4 * kind, scales)
 
         xp_plane = tile("xp_plane", [P, S], U8)
-        xp_codes = tile("xp_codes", [P, S], U32)
-        nc.vector.tensor_copy(out=xp_codes[:], in_=x_codes[:].indirect(offs_sb[:]))
+        xp_codes = [tile("xp_codes%d" % first, [P, count], U32) for first, count in PARTS]
         nc.vector.tensor_copy(out=xp_plane[:], in_=x_plane[:].indirect(offs_sb[:]))
 
         w1_bf = tile("w1_bf", [P, PACK, P, PACK], BF16)
-
-        def w1_views(b, m0, m1):
-            dst = w1_bf[:, :, GROUPS * b + m0 : GROUPS * b + m1, :].rearrange("p t m j -> p m t j")
-            src = w1_raw[b][:, :, PACK * m0 : PACK * m1].rearrange("p j (m t) -> p m t j", t=PACK)
-            return dst, src
-
-        dst, src = w1_views(0, 0, GROUPS)
-        nc.scalar.activation(out=dst, in_=src, func=COPY)
-        dst, src = w1_views(1, 0, GROUPS_VECTOR)
-        nc.vector.tensor_copy(out=dst, in_=src)
-        dst, src = w1_views(1, GROUPS_VECTOR, GROUPS)
-        nc.scalar.copy(out=dst, in_=src)
-
-        w1_codes = tile("w1_codes", [P, H], U32)
+        first_codes = tile("first_codes", [P, P], U32)
+        later_codes = tile("later_codes", [P, H - P], U32, "x_codes")
+        w1_codes = [first_codes[:]] + [later_codes[:, P * n : P * (n + 1)] for n in range(PACK - 1)]
         w1_plane = tile("w1_plane", [P, H], U8)
-        h_first = [tile("h%d" % t, [P, S], F32) for t in range(2)]
-        h_second = tile("h23", [P, 2, S], F32)
-        h = [h_first[0][:], h_first[1][:], h_second[:, 0], h_second[:, 1]]
-        for t in range(PACK):
+
+        def round_w1(copy, b, t0, t1):
+            copy(
+                out=w1_bf[:, t0:t1, GROUPS * b : GROUPS * (b + 1), :].rearrange("p t m j -> p m t j"),
+                in_=w1_raw[b][:].rearrange("p j (m t) -> p m t j", t=PACK)[:, :, t0:t1, :],
+            )
+
+        def quantise_w1(t):
             cols = slice(P * t, P * (t + 1))
             nc.vector.quantize_mx(
-                out=w1_codes[:, cols].bitcast(FP8X4),
+                out=w1_codes[t].bitcast(FP8X4),
                 scales=w1_plane[:, cols],
                 in_=w1_bf[:, t].rearrange("p m j -> p (m j)"),
             )
 
-        def first_pass(t, out, picked):
+        def first_pass(t, out, part):
             cols = slice(P * t, P * (t + 1))
+            first, count = PARTS[part]
             nc.tensor.matmul_mx(
                 out=out,
-                lhsT=w1_codes[:, cols].bitcast(FP8X4),
+                lhsT=w1_codes[t].bitcast(FP8X4),
                 lhsT_scale=w1_plane[:, cols],
-                rhs=xp_codes[:, picked].bitcast(FP8X4),
-                rhs_scale=xp_plane[:, picked],
+                rhs=xp_codes[part][:].bitcast(FP8X4),
+                rhs_scale=xp_plane[:, first : first + count],
                 start=True,
                 stop=True,
             )
 
-        for part, number in enumerate((0, 7, 6, 5)):
-            picked = slice(P * part, P * (part + 1))
-            acc = bank(number, "h_acc0%d" % part)
-            first_pass(0, acc[:, 0:P], picked)
-            copy = nc.scalar.copy if part % 2 else nc.vector.tensor_copy
-            copy(out=h[0][:, picked], in_=acc[:, 0:P])
+        round_w1(lambda out, in_: nc.scalar.activation(out=out, in_=in_, func=COPY), 0, 0, PACK)
+        round_w1(nc.vector.tensor_copy, 1, 0, 1)
+        round_w1(nc.scalar.copy, 1, 1, PACK)
+        quantise_w1(0)
+
+        h_first = [tile("h%d" % t, [P, S], F32) for t in range(2)]
+        h_second = tile("h23", [P, 2, S], F32)
+        h = [h_first[0][:], h_first[1][:], h_second[:, 0], h_second[:, 1]]
+        for part, (first, count) in enumerate(PARTS):
+            nc.vector.tensor_copy(
+                out=xp_codes[part][:], in_=x_codes[:].indirect(offs_sb[:, first // 16 : (first + count) // 16])
+            )
+            acc = bank((0, 7, 6)[part], "h_acc0%d" % part)
+            first_pass(0, acc[:, 0:count], part)
+            nc.scalar.copy(out=h[0][:, first : first + count], in_=acc[:, 0:count])
+        for t in range(1, PACK):
+            quantise_w1(t)
         acc = bank(1, "h_acc1")
-        first_pass(1, acc[:], slice(0, S))
+        for part, (first, count) in enumerate(PARTS):
+            first_pass(1, acc[:, first : first + count], part)
         nc.scalar.copy(out=h[1], in_=acc[:])
-        for part in range(2):
-            picked = slice(S // 2 * part, S // 2 * (part + 1))
-            acc = bank(2 + part, "h_acc23%d" % part)
+        for half, parts in enumerate(((0,), (1, 2))):
+            picked = slice(S // 2 * half, S // 2 * (half + 1))
+            acc = bank(2 + half, "h_acc23%d" % half)
             for e in range(2):
-                first_pass(2 + e, acc[:, S // 2 * e : S // 2 * (e + 1)], picked)
+                for part in parts:
+                    first, count = PARTS[part]
+                    place = S // 2 * e + first - picked.start
+                    first_pass(2 + e, acc[:, place : place + count], part)
             nc.scalar.copy(out=h_second[:, :, picked], in_=acc[:].rearrange("p (e n) -> p e n", e=2))
 
         wd_codes = [
             tile("wd_codes%d" % kind, [P, H], U32, after)
-            for kind, after in enumerate(("w1_bf", "w1_codes", "w1_plane"))
+            for kind, after in enumerate(("w1_bf", "x_codes", "w1_plane"))
         ]
         wd_plane = tile("wd_plane", [P, H], U8)
         y_codes = tile("y_codes", [P, V], U32)

@@ -21,7 +21,6 @@ PACK = 4
 LISTS = 3
 HALF = V // 2
 LINE = 4
-GROUPS = P // 2
 PARTS = ((0, 256), (256, 128), (384, 128))
 MEAN, LARGEST, SMALLEST = 0, 1, 2
 EXTREME_OP = {LARGEST: ALU.max, SMALLEST: ALU.min}
@@ -60,7 +59,7 @@ def tile_picked_pna_none_po_kernel(
         pos_sb = [tile("pos_sb%d" % d, [P, V // 16], U16) for d in range(LISTS)]
         x_plane = tile("x_plane", [P, T], U8)
         x_codes = tile("x_codes", [P, T], U32)
-        w1_raw = [tile("w1_raw%d" % b, [P, PACK, H // 2], F32) for b in range(2)]
+        w1_raw = tile("w1_raw", [P, PACK, H], F32)
         w_codes = [tile("w_codes%d" % kind, [P, H], U32) for kind in range(3)]
         w_plane = tile("w_plane", [P, H], U8)
         identity = tile("identity", [P, P], F32)
@@ -70,10 +69,10 @@ def tile_picked_pna_none_po_kernel(
         make_identity(nc, identity[:])
 
         w1_rows = w1.rearrange("(p j) c -> p j c", j=PACK)
+        nc.sync.dma_start(out=w1_raw[:, 0:2, :], in_=w1_rows[:, 0:2, :])
         nc.sync.dma_start(out=offs_sb[:], in_=offs)
-        nc.sync.dma_start(out=w1_raw[0][:], in_=w1_rows[:, :, 0 : H // 2])
         load_scale_rows(nc, x_plane, 0, x_scales)
-        nc.sync.dma_start(out=w1_raw[1][:], in_=w1_rows[:, :, H // 2 : H])
+        nc.sync.dma_start(out=w1_raw[:, 2:4, :], in_=w1_rows[:, 2:4, :])
         nc.sync.dma_start(out=x_codes[:].bitcast(I32), in_=as_words(x_words))
         for d, pos in enumerate((pos1, pos2, pos3)):
             nc.sync.dma_start(out=pos_sb[d][:], in_=pos)
@@ -92,11 +91,10 @@ def tile_picked_pna_none_po_kernel(
         w1_codes = [first_codes[:]] + [later_codes[:, P * n : P * (n + 1)] for n in range(PACK - 1)]
         w1_plane = tile("w1_plane", [P, H], U8)
 
-        def round_w1(copy, b, t0, t1):
-            copy(
-                out=w1_bf[:, t0:t1, GROUPS * b : GROUPS * (b + 1), :].rearrange("p t m j -> p m t j"),
-                in_=w1_raw[b][:].rearrange("p j (m t) -> p m t j", t=PACK)[:, :, t0:t1, :],
-            )
+        def w1_views(t0, t1, j0=0, j1=PACK):
+            dst = w1_bf[:, t0:t1, :, j0:j1].rearrange("p t m j -> p m t j")
+            src = w1_raw[:, j0:j1, :].rearrange("p j (m t) -> p m t j", t=PACK)[:, :, t0:t1, :]
+            return dst, src
 
         def quantise_w1(t):
             cols = slice(P * t, P * (t + 1))
@@ -119,9 +117,12 @@ def tile_picked_pna_none_po_kernel(
                 stop=True,
             )
 
-        round_w1(lambda out, in_: nc.scalar.activation(out=out, in_=in_, func=COPY), 0, 0, PACK)
-        round_w1(nc.vector.tensor_copy, 1, 0, 1)
-        round_w1(nc.scalar.copy, 1, 1, PACK)
+        dst, src = w1_views(0, PACK, 0, 2)
+        nc.scalar.activation(out=dst, in_=src, func=COPY)
+        dst, src = w1_views(0, 1, 2, PACK)
+        nc.vector.tensor_copy(out=dst, in_=src)
+        dst, src = w1_views(1, PACK, 2, PACK)
+        nc.scalar.copy(out=dst, in_=src)
         quantise_w1(0)
 
         h_first = [tile("h%d" % t, [P, S], F32) for t in range(2)]

@@ -60,7 +60,7 @@ def tile_picked_pna_none_po_kernel(
         x_plane = tile("x_plane", [P, T], U8)
         x_codes = tile("x_codes", [P, T], U32)
         w1_raw = tile("w1_raw", [P, PACK, H], F32)
-        w_codes = [tile("w_codes%d" % kind, [P, H], U32) for kind in range(3)]
+        w_codes = tile("w_codes", [P, 3, H], U32)
         w_plane = tile("w_plane", [P, H], U8)
         identity = tile("identity", [P, P], F32)
 
@@ -77,7 +77,7 @@ def tile_picked_pna_none_po_kernel(
         for d, pos in enumerate((pos1, pos2, pos3)):
             nc.sync.dma_start(out=pos_sb[d][:], in_=pos)
         for kind, words in enumerate((w2_words, w3_words, w4_words)):
-            nc.sync.dma_start(out=w_codes[kind][:].bitcast(I32), in_=as_words(words))
+            nc.sync.dma_start(out=w_codes[:, kind, :].bitcast(I32), in_=as_words(words))
         for kind, scales in enumerate((w2_scales, w3_scales, w4_scales)):
             load_scale_rows(nc, w_plane, 4 * kind, scales)
 
@@ -151,10 +151,7 @@ def tile_picked_pna_none_po_kernel(
                     first_pass(2 + e, acc[:, place : place + count], part)
             nc.scalar.copy(out=h_second[:, :, picked], in_=acc[:].rearrange("p (e n) -> p e n", e=2))
 
-        wd_codes = [
-            tile("wd_codes%d" % kind, [P, H], U32, after)
-            for kind, after in enumerate(("w1_bf", "x_codes", "w1_plane"))
-        ]
+        wd_codes = tile("wd_codes", [P, 3, H], U32, "w1_bf")
         wd_plane = tile("wd_plane", [P, H], U8)
         y_codes = tile("y_codes", [P, V], U32)
         y_plane = tile("y_plane", [P, V], U8)
@@ -162,11 +159,10 @@ def tile_picked_pna_none_po_kernel(
         out_words = as_words(out_1)
 
         def deal_weights():
-            for kind in range(3):
-                nc.gpsimd.tensor_copy(
-                    out=wd_codes[kind][:].bitcast(I32).rearrange("p (t m) -> p t m", t=PACK),
-                    in_=w_codes[kind][:].bitcast(I32).rearrange("p (m t) -> p t m", t=PACK),
-                )
+            nc.gpsimd.tensor_copy(
+                out=wd_codes[:].bitcast(I32).rearrange("p k (t m) -> p k t m", t=PACK),
+                in_=w_codes[:].bitcast(I32).rearrange("p k (m t) -> p k t m", t=PACK),
+            )
             nc.gpsimd.tensor_copy(
                 out=wd_plane[:].rearrange("p (t m) -> p t m", t=PACK),
                 in_=w_plane[:].rearrange("p (m t) -> p t m", t=PACK),
@@ -270,7 +266,7 @@ def tile_picked_pna_none_po_kernel(
                 place = t % per_bank
                 nc.tensor.matmul_mx(
                     out=acc[t // per_bank][:, HALF * place : HALF * (place + 1)],
-                    lhsT=wd_codes[kind][:, cols].bitcast(FP8X4),
+                    lhsT=wd_codes[:, kind, cols].bitcast(FP8X4),
                     lhsT_scale=wd_plane[4 * kind : P, cols],
                     rhs=z_codes[:].bitcast(FP8X4),
                     rhs_scale=z_plane[:],

@@ -125,9 +125,7 @@ def tile_picked_pna_none_po_kernel(
         nc.scalar.copy(out=dst, in_=src)
         quantise_w1(0)
 
-        h_first = [tile("h%d" % t, [P, S], F32) for t in range(2)]
-        h_second = tile("h23", [P, 2, S], F32)
-        h = [h_first[0][:], h_first[1][:], h_second[:, 0], h_second[:, 1]]
+        h = [tile("h%d" % t, [P, S], F32) for t in range(PACK)]
         for part, (first, count) in enumerate(PARTS):
             nc.vector.tensor_copy(
                 out=xp_codes[part][:], in_=x_codes[:].indirect(offs_sb[:, first // 16 : (first + count) // 16])
@@ -137,19 +135,11 @@ def tile_picked_pna_none_po_kernel(
             nc.scalar.copy(out=h[0][:, first : first + count], in_=acc[:, 0:count])
         for t in range(1, PACK):
             quantise_w1(t)
-        acc = bank(1, "h_acc1")
-        for part, (first, count) in enumerate(PARTS):
-            first_pass(1, acc[:, first : first + count], part)
-        nc.scalar.copy(out=h[1], in_=acc[:])
-        for half, parts in enumerate(((0,), (1, 2))):
-            picked = slice(S // 2 * half, S // 2 * (half + 1))
-            acc = bank(2 + half, "h_acc23%d" % half)
-            for e in range(2):
-                for part in parts:
-                    first, count = PARTS[part]
-                    place = S // 2 * e + first - picked.start
-                    first_pass(2 + e, acc[:, place : place + count], part)
-            nc.scalar.copy(out=h_second[:, :, picked], in_=acc[:].rearrange("p (e n) -> p e n", e=2))
+        for t in range(1, PACK):
+            acc = bank(t, "h_acc%d" % t)
+            for part, (first, count) in enumerate(PARTS):
+                first_pass(t, acc[:, first : first + count], part)
+            nc.scalar.copy(out=h[t][:], in_=acc[:])
 
         wd_codes = tile("wd_codes", [P, 3, H], U32, "w1_bf")
         wd_plane = tile("wd_plane", [P, H], U8)
@@ -168,68 +158,50 @@ def tile_picked_pna_none_po_kernel(
                 in_=w_plane[:].rearrange("p (m t) -> p t m", t=PACK),
             )
 
-        rounded = [tile("rounded%d" % d, [P, 2, V, 2], BF16) for d in range(LISTS)]
-        of_two = [{kind: tile("of_two%d%d" % (a, kind), [P, 2, HALF, 2], BF16) for kind in EXTREME_OP} for a in range(2)]
+        fetched = [tile("fetched%d" % d, [P, PACK, V], F32) for d in range(LISTS)]
+        rounded = [[tile("rounded%d%d" % (a, d), [P, HALF * PACK], BF16) for d in range(LISTS)] for a in range(2)]
+        of_two = [{kind: tile("of_two%d%d" % (a, kind), [P, HALF * PACK], BF16) for kind in EXTREME_OP} for a in range(2)]
+        sums = [bank(4 + a, "sums%d" % a) for a in range(2)]
         mean_back = [bank(6 + a, "mean_back%d" % a) for a in range(2)]
 
-        def add_turned(sums, e, values, start, stop):
+        def add_turned(a, t, d):
             nc.tensor.matmul(
-                out=sums[:, P * e : P * (e + 1)], lhsT=values, rhs=identity[:], is_transpose=True, start=start, stop=stop
+                out=sums[a][:, P * t : P * (t + 1)], lhsT=fetched[d][:, t, half_of_targets(a)], rhs=identity[:],
+                is_transpose=True, start=(t, d) == (0, 0), stop=(t, d) == (PACK - 1, LISTS - 1),
             )
 
-        def round_mean(u, a, sums):
-            turned = tile("turned%d%d" % (a, u), [P, P, 2], BF16)
+        def fetch_on_vector(t, d):
+            nc.vector.tensor_copy(out=fetched[d][:, t, :], in_=h[t][:].indirect(pos_sb[d][:]))
+            for a in range(2):
+                add_turned(a, t, d)
+
+        def fetch_on_scalar(t, d, halves):
+            first, last = HALF * halves[0], HALF * (halves[-1] + 1)
+            offsets = pos_sb[d][:, first // 16 : last // 16]
+            nc.scalar.activation(out=fetched[d][:, t, first:last], in_=h[t][:].indirect(offsets), func=COPY)
+            for a in halves:
+                add_turned(a, t, d)
+
+        def round_mean(a):
+            turned = tile("turned%d" % a, [P, 2, P, 2], BF16)
             nc.scalar.activation(
                 out=turned[:],
-                in_=sums.rearrange("v (e p) -> v p e", e=2),
+                in_=sums[a][:].rearrange("v (u e p) -> v u p e", u=2, e=2),
                 func=COPY,
                 scale=1.0 / LISTS,
             )
-            nc.tensor.transpose(
-                mean_back[a][:, P * u : P * (u + 1)], turned[:].rearrange("v p e -> v (p e)").bitcast(F32), identity[:]
+            for u in range(2):
+                nc.tensor.transpose(
+                    mean_back[a][:, P * u : P * (u + 1)],
+                    turned[:, u].rearrange("v p e -> v (p e)").bitcast(F32),
+                    identity[:],
+                )
+
+        def round_list(copy, a, d):
+            copy(
+                out=rounded[a][d][:].rearrange("p (c i t) -> p c t i", i=LINE, t=PACK),
+                in_=fetched[d][:, :, half_of_targets(a)].rearrange("p t (c i) -> p c t i", i=LINE),
             )
-
-        def round_pair(d, u, fetched, first):
-            nc.scalar.copy(
-                out=rounded[d][:, u, first : first + fetched.shape[2], :].rearrange("p (c i) e -> p c e i", i=LINE),
-                in_=fetched.rearrange("p e (c i) -> p c e i", i=LINE),
-            )
-
-        def fetch_first_pair():
-            both = bank(4, "sums0")
-            sums = [both[:, 2 * P * a : 2 * P * (a + 1)] for a in range(2)]
-            fetched = [tile("fetched%d0" % d, [P, 2, V], F32) for d in range(LISTS)]
-            for e in range(2):
-                for d in range(LISTS):
-                    nc.vector.tensor_copy(out=fetched[d][:, e, :], in_=h[e].indirect(pos_sb[d][:]))
-                    for a in range(2):
-                        add_turned(
-                            sums[a], e, fetched[d][:, e, half_of_targets(a)],
-                            (e, d, a) == (0, 0, 0), (e, d, a) == (1, LISTS - 1, 1),
-                        )
-                    if e == 1:
-                        round_pair(d, 0, fetched[d][:], 0)
-            for a in range(2):
-                round_mean(0, a, sums[a])
-
-        def fetch_second_pair():
-            held = [bank(number, "sums1%d" % a) for a, number in enumerate((5, 3))]
-            sums = [held[a][:, 0 : 2 * P] for a in range(2)]
-            fetched = [tile("fetched%d1" % d, [P, 2, V], F32) for d in range(LISTS)]
-            for d in range(LISTS):
-                for e in range(2):
-                    last = (d, e) == (LISTS - 1, 1)
-                    if not last:
-                        nc.vector.tensor_copy(out=fetched[d][:, e, :], in_=h[2 + e].indirect(pos_sb[d][:]))
-                    for a in range(2):
-                        values = fetched[d][:, e, half_of_targets(a)]
-                        if last:
-                            offsets = pos_sb[d][:, HALF // 16 * a : HALF // 16 * (a + 1)]
-                            nc.vector.tensor_copy(out=values, in_=h[2 + e].indirect(offsets))
-                        add_turned(sums[a], e, values, (d, e) == (0, 0), last)
-                if d < LISTS - 1:
-                    round_pair(d, 1, fetched[d][:], 0)
-            return sums, fetched[LISTS - 1]
 
         z_bf = [[tile("z_bf%d%d" % (a, kind), [P, HALF * PACK], BF16) for kind in range(3)] for a in range(2)]
 
@@ -240,20 +212,13 @@ def tile_picked_pna_none_po_kernel(
             )
 
         def extreme_of_two(a, kind):
-            targets = half_of_targets(a)
             nc.vector.tensor_tensor(
-                out=of_two[a][kind][:],
-                in0=rounded[0][:, :, targets, :],
-                in1=rounded[1][:, :, targets, :],
-                op=EXTREME_OP[kind],
+                out=of_two[a][kind][:], in0=rounded[a][0][:], in1=rounded[a][1][:], op=EXTREME_OP[kind]
             )
 
         def extreme_of_three(a, kind):
             nc.vector.tensor_tensor(
-                out=z_bf[a][kind][:].rearrange("p (v u e) -> p v u e", u=2, e=2),
-                in0=of_two[a][kind][:].rearrange("p u v e -> p v u e"),
-                in1=rounded[2][:, :, half_of_targets(a), :].rearrange("p u v e -> p v u e"),
-                op=EXTREME_OP[kind],
+                out=z_bf[a][kind][:], in0=of_two[a][kind][:], in1=rounded[a][2][:], op=EXTREME_OP[kind]
             )
 
         def second_product(a, kind, acc, kinds):
@@ -297,29 +262,39 @@ def tile_picked_pna_none_po_kernel(
             )
             nc.sync.dma_start(out=out_words[:, targets], in_=y_codes[:, targets].bitcast(I32))
 
-        fetch_first_pair()
+        for t in range(2):
+            for d in range(LISTS):
+                fetch_on_vector(t, d)
         deal_weights()
-        sums, last_fetched = fetch_second_pair()
-        round_pair(LISTS - 1, 1, last_fetched[:, :, half_of_targets(0)], 0)
-        round_mean(1, 0, sums[0])
-        round_mean(1, 1, sums[1])
-        round_pair(LISTS - 1, 1, last_fetched[:, :, half_of_targets(1)], HALF)
+        for d in range(LISTS - 1):
+            for t in range(2, PACK):
+                fetch_on_scalar(t, d, (0, 1))
+        fetch_on_vector(2, LISTS - 1)
+        for a in range(2):
+            fetch_on_scalar(PACK - 1, LISTS - 1, (a,))
+        round_mean(0)
+        round_mean(1)
         lay_mean(0)
         lay_mean(1)
+        round_list(nc.scalar.copy, 1, 0)
         acc_first = [bank(number, "y_acc0%d" % number) for number in (0, 1)]
-        acc_second = [bank(number, "y_acc1%d" % number) for number in (2, 4, 5, 3)]
+        acc_second = [bank(number, "y_acc1%d" % number) for number in (2, 3, 4, 5)]
         kinds_first, kinds_second = (LARGEST, SMALLEST, MEAN), (MEAN, LARGEST, SMALLEST)
+        for d in range(LISTS):
+            round_list(nc.vector.tensor_copy, 0, d)
         extreme_of_two(0, LARGEST)
         extreme_of_two(0, SMALLEST)
         extreme_of_three(0, LARGEST)
         extreme_of_three(0, SMALLEST)
         second_product(0, LARGEST, acc_first, kinds_first)
         second_product(0, SMALLEST, acc_first, kinds_first)
+        round_list(nc.vector.tensor_copy, 1, 1)
+        second_product(0, MEAN, acc_first, kinds_first)
+        round_list(nc.vector.tensor_copy, 1, 2)
         extreme_of_two(1, LARGEST)
         extreme_of_two(1, SMALLEST)
-        second_product(0, MEAN, acc_first, kinds_first)
-        extreme_of_three(1, LARGEST)
         second_product(1, MEAN, acc_second, kinds_second)
+        extreme_of_three(1, LARGEST)
         extreme_of_three(1, SMALLEST)
         second_product(1, LARGEST, acc_second, kinds_second)
         second_product(1, SMALLEST, acc_second, kinds_second)

@@ -82,7 +82,7 @@ def tile_picked_pna_none_po_kernel(
             load_scale_rows(nc, w_plane, 4 * kind, scales)
 
         xp_plane = tile("xp_plane", [P, S], U8)
-        xp_codes = [tile("xp_codes%d" % first, [P, count], U32) for first, count in PARTS]
+        xp_codes = tile("xp_codes", [P, S], U32)
         nc.vector.tensor_copy(out=xp_plane[:], in_=x_plane[:].indirect(offs_sb[:]))
 
         w1_bf = tile("w1_bf", [P, PACK, P, PACK], BF16)
@@ -104,14 +104,13 @@ def tile_picked_pna_none_po_kernel(
                 in_=w1_bf[:, t].rearrange("p m j -> p (m j)"),
             )
 
-        def first_pass(t, out, part):
+        def first_pass(t, out, first, count):
             cols = slice(P * t, P * (t + 1))
-            first, count = PARTS[part]
             nc.tensor.matmul_mx(
                 out=out,
                 lhsT=w1_codes[t].bitcast(FP8X4),
                 lhsT_scale=w1_plane[:, cols],
-                rhs=xp_codes[part][:].bitcast(FP8X4),
+                rhs=xp_codes[:, first : first + count].bitcast(FP8X4),
                 rhs_scale=xp_plane[:, first : first + count],
                 start=True,
                 stop=True,
@@ -128,17 +127,17 @@ def tile_picked_pna_none_po_kernel(
         h = [tile("h%d" % t, [P, S], F32) for t in range(PACK)]
         for part, (first, count) in enumerate(PARTS):
             nc.vector.tensor_copy(
-                out=xp_codes[part][:], in_=x_codes[:].indirect(offs_sb[:, first // 16 : (first + count) // 16])
+                out=xp_codes[:, first : first + count],
+                in_=x_codes[:].indirect(offs_sb[:, first // 16 : (first + count) // 16]),
             )
             acc = bank((0, 7, 6)[part], "h_acc0%d" % part)
-            first_pass(0, acc[:, 0:count], part)
+            first_pass(0, acc[:, 0:count], first, count)
             nc.scalar.copy(out=h[0][:, first : first + count], in_=acc[:, 0:count])
         for t in range(1, PACK):
             quantise_w1(t)
         for t in range(1, PACK):
             acc = bank(t, "h_acc%d" % t)
-            for part, (first, count) in enumerate(PARTS):
-                first_pass(t, acc[:, first : first + count], part)
+            first_pass(t, acc[:], 0, S)
             nc.scalar.copy(out=h[t][:], in_=acc[:])
 
         wd_codes = tile("wd_codes", [P, 3, H], U32, "w1_bf")
@@ -159,7 +158,8 @@ def tile_picked_pna_none_po_kernel(
             )
 
         fetched = [tile("fetched%d" % d, [P, PACK, V], F32) for d in range(LISTS)]
-        rounded = [[tile("rounded%d%d" % (a, d), [P, HALF * PACK], BF16) for d in range(LISTS)] for a in range(2)]
+        all_rounded = tile("all_rounded", [P, 2, LISTS, HALF * PACK], BF16, "w_codes")
+        rounded = [[all_rounded[:, a, d] for d in range(LISTS)] for a in range(2)]
         of_two = [{kind: tile("of_two%d%d" % (a, kind), [P, HALF * PACK], BF16) for kind in EXTREME_OP} for a in range(2)]
         sums = [bank(4 + a, "sums%d" % a) for a in range(2)]
         mean_back = [bank(6 + a, "mean_back%d" % a) for a in range(2)]
@@ -170,9 +170,11 @@ def tile_picked_pna_none_po_kernel(
                 is_transpose=True, start=(t, d) == (0, 0), stop=(t, d) == (PACK - 1, LISTS - 1),
             )
 
-        def fetch_on_vector(t, d):
-            nc.vector.tensor_copy(out=fetched[d][:, t, :], in_=h[t][:].indirect(pos_sb[d][:]))
-            for a in range(2):
+        def fetch_on_vector(t, d, halves):
+            first, last = HALF * halves[0], HALF * (halves[-1] + 1)
+            offsets = pos_sb[d][:, first // 16 : last // 16]
+            nc.vector.tensor_copy(out=fetched[d][:, t, first:last], in_=h[t][:].indirect(offsets))
+            for a in halves:
                 add_turned(a, t, d)
 
         def fetch_on_scalar(t, d, halves):
@@ -199,7 +201,7 @@ def tile_picked_pna_none_po_kernel(
 
         def round_list(copy, a, d):
             copy(
-                out=rounded[a][d][:].rearrange("p (c i t) -> p c t i", i=LINE, t=PACK),
+                out=rounded[a][d].rearrange("p (c i t) -> p c t i", i=LINE, t=PACK),
                 in_=fetched[d][:, :, half_of_targets(a)].rearrange("p t (c i) -> p c t i", i=LINE),
             )
 
@@ -213,17 +215,18 @@ def tile_picked_pna_none_po_kernel(
 
         def extreme_of_two(a, kind):
             nc.vector.tensor_tensor(
-                out=of_two[a][kind][:], in0=rounded[a][0][:], in1=rounded[a][1][:], op=EXTREME_OP[kind]
+                out=of_two[a][kind][:], in0=rounded[a][0], in1=rounded[a][1], op=EXTREME_OP[kind]
             )
 
         def extreme_of_three(a, kind):
             nc.vector.tensor_tensor(
-                out=z_bf[a][kind][:], in0=of_two[a][kind][:], in1=rounded[a][2][:], op=EXTREME_OP[kind]
+                out=z_bf[a][kind][:], in0=of_two[a][kind][:], in1=rounded[a][2], op=EXTREME_OP[kind]
             )
 
         def second_product(a, kind, acc, kinds):
             per_bank = PACK // len(acc)
-            z_codes = tile("z_codes%d%d" % (a, kind), [P, HALF], U32)
+            after = ("z_bf0%d" % SMALLEST, "of_two1%d" % LARGEST)[a] if kind == MEAN else ""
+            z_codes = tile("z_codes%d%d" % (a, kind), [P, HALF], U32, after)
             z_plane = tile("z_plane%d%d" % (a, kind), [P, HALF], U8)
             nc.vector.quantize_mx(out=z_codes[:].bitcast(FP8X4), scales=z_plane[:], in_=z_bf[a][kind][:])
             for t in range(PACK):
@@ -264,40 +267,41 @@ def tile_picked_pna_none_po_kernel(
 
         for t in range(2):
             for d in range(LISTS):
-                fetch_on_vector(t, d)
+                fetch_on_vector(t, d, (0, 1))
         deal_weights()
         for d in range(LISTS - 1):
             for t in range(2, PACK):
                 fetch_on_scalar(t, d, (0, 1))
-        fetch_on_vector(2, LISTS - 1)
+        fetch_on_vector(2, LISTS - 1, (0, 1))
         for a in range(2):
             fetch_on_scalar(PACK - 1, LISTS - 1, (a,))
         round_mean(0)
         round_mean(1)
         lay_mean(0)
         lay_mean(1)
-        round_list(nc.scalar.copy, 1, 0)
         acc_first = [bank(number, "y_acc0%d" % number) for number in (0, 1)]
         acc_second = [bank(number, "y_acc1%d" % number) for number in (2, 3, 4, 5)]
-        kinds_first, kinds_second = (LARGEST, SMALLEST, MEAN), (MEAN, LARGEST, SMALLEST)
-        for d in range(LISTS):
-            round_list(nc.vector.tensor_copy, 0, d)
+        kinds = (LARGEST, SMALLEST, MEAN)
+        for a in range(2):
+            for d in range(LISTS - 1):
+                round_list(nc.vector.tensor_copy, a, d)
+        round_list(nc.vector.tensor_copy, 0, LISTS - 1)
         extreme_of_two(0, LARGEST)
         extreme_of_two(0, SMALLEST)
         extreme_of_three(0, LARGEST)
         extreme_of_three(0, SMALLEST)
-        second_product(0, LARGEST, acc_first, kinds_first)
-        second_product(0, SMALLEST, acc_first, kinds_first)
-        round_list(nc.vector.tensor_copy, 1, 1)
-        second_product(0, MEAN, acc_first, kinds_first)
-        round_list(nc.vector.tensor_copy, 1, 2)
+        second_product(0, LARGEST, acc_first, kinds)
+        second_product(0, SMALLEST, acc_first, kinds)
         extreme_of_two(1, LARGEST)
+        round_list(nc.vector.tensor_copy, 1, LISTS - 1)
+        second_product(0, MEAN, acc_first, kinds)
         extreme_of_two(1, SMALLEST)
-        second_product(1, MEAN, acc_second, kinds_second)
         extreme_of_three(1, LARGEST)
+        kinds = (MEAN, LARGEST, SMALLEST)
+        second_product(1, MEAN, acc_second, kinds)
+        second_product(1, LARGEST, acc_second, kinds)
         extreme_of_three(1, SMALLEST)
-        second_product(1, LARGEST, acc_second, kinds_second)
-        second_product(1, SMALLEST, acc_second, kinds_second)
+        second_product(1, SMALLEST, acc_second, kinds)
 
         y_first = store_values(0, acc_first, [nc.scalar.copy] * 2)
         store_codes(0, y_first, "z_bf%d%d" % (1, SMALLEST))

@@ -265,14 +265,15 @@ def tile_picked_pna_none_po_kernel(
             )
             nc.sync.dma_start(out=out_words[:, targets], in_=y_codes[:, targets].bitcast(I32))
 
-        for t in range(2):
-            for d in range(LISTS):
-                fetch_on_vector(t, d, (0, 1))
         deal_weights()
-        for d in range(LISTS - 1):
-            for t in range(2, PACK):
-                fetch_on_scalar(t, d, (0, 1))
-        fetch_on_vector(2, LISTS - 1, (0, 1))
+        both = (0, 1)
+        for d in range(LISTS):
+            fetch_on_vector(0, d, both)
+        for d in range(LISTS):
+            fetch_on_vector(1, d, both)
+            fetch_on_scalar(2 + d % 2, d // 2, both)
+        fetch_on_vector(2, LISTS - 1, both)
+        fetch_on_scalar(PACK - 1, 1, both)
         for a in range(2):
             fetch_on_scalar(PACK - 1, LISTS - 1, (a,))
         round_mean(0)

@@ -64,12 +64,12 @@ def tile_picked_pna_none_po_kernel(
         w_plane = tile("w_plane", [P, H], U8)
         identity = tile("identity", [P, P], F32)
 
-        nc.vector.memset(x_plane[:].bitcast(I32), 0)
+        nc.gpsimd.memset(x_plane[:].bitcast(I32), 0)
         nc.gpsimd.memset(w_plane[:].bitcast(I32), 0)
         make_identity(nc, identity[:])
 
         w1_rows = w1.rearrange("(p j) c -> p j c", j=PACK)
-        nc.sync.dma_start(out=w1_raw[:, 0:2, :], in_=w1_rows[:, 0:2, :])
+        nc.scalar.dma_start(out=w1_raw[:, 0:2, :], in_=w1_rows[:, 0:2, :])
         nc.sync.dma_start(out=offs_sb[:], in_=offs)
         load_scale_rows(nc, x_plane, 0, x_scales)
         nc.sync.dma_start(out=w1_raw[:, 2:4, :], in_=w1_rows[:, 2:4, :])
@@ -86,9 +86,9 @@ def tile_picked_pna_none_po_kernel(
         nc.vector.tensor_copy(out=xp_plane[:], in_=x_plane[:].indirect(offs_sb[:]))
 
         w1_bf = tile("w1_bf", [P, PACK, P, PACK], BF16)
-        first_codes = tile("first_codes", [P, P], U32)
-        later_codes = tile("later_codes", [P, H - P], U32, "x_codes")
-        w1_codes = [first_codes[:]] + [later_codes[:, P * n : P * (n + 1)] for n in range(PACK - 1)]
+        early_codes = tile("early_codes", [P, H // 2], U32)
+        later_codes = tile("later_codes", [P, H // 2], U32, "x_codes")
+        w1_codes = [(early_codes, later_codes)[t // 2][:, P * (t % 2) : P * (t % 2 + 1)] for t in range(PACK)]
         w1_plane = tile("w1_plane", [P, H], U8)
 
         def w1_views(t0, t1, j0=0, j1=PACK):
@@ -118,13 +118,16 @@ def tile_picked_pna_none_po_kernel(
 
         dst, src = w1_views(0, PACK, 0, 2)
         nc.scalar.activation(out=dst, in_=src, func=COPY)
-        dst, src = w1_views(0, 1, 2, PACK)
-        nc.vector.tensor_copy(out=dst, in_=src)
-        dst, src = w1_views(1, PACK, 2, PACK)
+        for t in range(2):
+            dst, src = w1_views(t, t + 1, 2, PACK)
+            nc.vector.tensor_copy(out=dst, in_=src)
+        dst, src = w1_views(2, PACK, 2, PACK)
         nc.scalar.copy(out=dst, in_=src)
         quantise_w1(0)
+        quantise_w1(1)
 
         h = [tile("h%d" % t, [P, S], F32) for t in range(PACK)]
+        acc1 = bank(1, "h_acc1")
         for part, (first, count) in enumerate(PARTS):
             nc.vector.tensor_copy(
                 out=xp_codes[:, first : first + count],
@@ -132,10 +135,14 @@ def tile_picked_pna_none_po_kernel(
             )
             acc = bank((0, 7, 6)[part], "h_acc0%d" % part)
             first_pass(0, acc[:, 0:count], first, count)
+            if part == 0:
+                first_pass(1, acc1[:, 0:count], first, count)
             nc.scalar.copy(out=h[0][:, first : first + count], in_=acc[:, 0:count])
-        for t in range(1, PACK):
-            quantise_w1(t)
-        for t in range(1, PACK):
+        quantise_w1(2)
+        quantise_w1(3)
+        first_pass(1, acc1[:, S // 2 : S], S // 2, S // 2)
+        nc.scalar.copy(out=h[1][:], in_=acc1[:])
+        for t in range(2, PACK):
             acc = bank(t, "h_acc%d" % t)
             first_pass(t, acc[:], 0, S)
             nc.scalar.copy(out=h[t][:], in_=acc[:])
@@ -167,7 +174,7 @@ def tile_picked_pna_none_po_kernel(
         def add_turned(a, t, d):
             nc.tensor.matmul(
                 out=sums[a][:, P * t : P * (t + 1)], lhsT=fetched[d][:, t, half_of_targets(a)], rhs=identity[:],
-                is_transpose=True, start=(t, d) == (0, 0), stop=(t, d) == (PACK - 1, LISTS - 1),
+                is_transpose=True, start=(t, d) == (0, 0), stop=(t, d) == (PACK - 1 - a, LISTS - 1),
             )
 
         def fetch_on_vector(t, d, halves):
@@ -272,10 +279,10 @@ def tile_picked_pna_none_po_kernel(
         for d in range(LISTS):
             fetch_on_vector(1, d, both)
             fetch_on_scalar(2 + d % 2, d // 2, both)
-        fetch_on_vector(2, LISTS - 1, both)
+        fetch_on_vector(2, LISTS - 1, (0,))
         fetch_on_scalar(PACK - 1, 1, both)
-        for a in range(2):
-            fetch_on_scalar(PACK - 1, LISTS - 1, (a,))
+        fetch_on_scalar(PACK - 1, LISTS - 1, both)
+        fetch_on_scalar(2, LISTS - 1, (1,))
         round_mean(0)
         round_mean(1)
         lay_mean(0)

@@ -69,7 +69,7 @@ def tile_picked_pna_none_po_kernel(
         make_identity(nc, identity[:])
 
         w1_rows = w1.rearrange("(p j) c -> p j c", j=PACK)
-        nc.scalar.dma_start(out=w1_raw[:, 0:2, :], in_=w1_rows[:, 0:2, :])
+        nc.sync.dma_start(out=w1_raw[:, 0:2, :], in_=w1_rows[:, 0:2, :])
         nc.sync.dma_start(out=offs_sb[:], in_=offs)
         load_scale_rows(nc, x_plane, 0, x_scales)
         nc.sync.dma_start(out=w1_raw[:, 2:4, :], in_=w1_rows[:, 2:4, :])
@@ -83,8 +83,6 @@ def tile_picked_pna_none_po_kernel(
 
         xp_plane = tile("xp_plane", [P, S], U8)
         xp_codes = tile("xp_codes", [P, S], U32)
-        nc.vector.tensor_copy(out=xp_plane[:], in_=x_plane[:].indirect(offs_sb[:]))
-
         w1_bf = tile("w1_bf", [P, PACK, P, PACK], BF16)
         early_codes = tile("early_codes", [P, H // 2], U32)
         later_codes = tile("later_codes", [P, H // 2], U32, "x_codes")
@@ -116,11 +114,15 @@ def tile_picked_pna_none_po_kernel(
                 stop=True,
             )
 
-        dst, src = w1_views(0, PACK, 0, 2)
+        dst, src = w1_views(1, PACK, 0, 2)
         nc.scalar.activation(out=dst, in_=src, func=COPY)
-        for t in range(2):
-            dst, src = w1_views(t, t + 1, 2, PACK)
-            nc.vector.tensor_copy(out=dst, in_=src)
+        dst, src = w1_views(0, 1, 0, 2)
+        nc.vector.tensor_copy(out=dst, in_=src)
+        nc.vector.tensor_copy(out=xp_plane[:], in_=x_plane[:].indirect(offs_sb[:]))
+        dst, src = w1_views(0, 1, 2, PACK)
+        nc.vector.tensor_copy(out=dst, in_=src)
+        dst, src = w1_views(1, 2, 2, PACK)
+        nc.scalar.copy(out=dst, in_=src)
         dst, src = w1_views(2, PACK, 2, PACK)
         nc.scalar.copy(out=dst, in_=src)
         quantise_w1(0)

@@ -167,8 +167,8 @@ def tile_picked_pna_none_po_kernel(
             )
 
         fetched = [tile("fetched%d" % d, [P, PACK, V], F32) for d in range(LISTS)]
-        all_rounded = tile("all_rounded", [P, 2, LISTS, HALF * PACK], BF16, "w_codes")
-        rounded = [[all_rounded[:, a, d] for d in range(LISTS)] for a in range(2)]
+        all_rounded = tile("all_rounded", [P, LISTS, 2, HALF * PACK], BF16, "w_codes")
+        rounded = [[all_rounded[:, d, a] for d in range(LISTS)] for a in range(2)]
         of_two = [{kind: tile("of_two%d%d" % (a, kind), [P, HALF * PACK], BF16) for kind in EXTREME_OP} for a in range(2)]
         sums = [bank(4 + a, "sums%d" % a) for a in range(2)]
         mean_back = [bank(6 + a, "mean_back%d" % a) for a in range(2)]
@@ -176,7 +176,7 @@ def tile_picked_pna_none_po_kernel(
         def add_turned(a, t, d):
             nc.tensor.matmul(
                 out=sums[a][:, P * t : P * (t + 1)], lhsT=fetched[d][:, t, half_of_targets(a)], rhs=identity[:],
-                is_transpose=True, start=(t, d) == (0, 0), stop=(t, d) == (PACK - 1 - a, LISTS - 1),
+                is_transpose=True, start=(t, d) == (0, 0), stop=(t, d) == (PACK - 1, LISTS - 1),
             )
 
         def fetch_on_vector(t, d, halves):
@@ -212,6 +212,12 @@ def tile_picked_pna_none_po_kernel(
             copy(
                 out=rounded[a][d].rearrange("p (c i t) -> p c t i", i=LINE, t=PACK),
                 in_=fetched[d][:, :, half_of_targets(a)].rearrange("p t (c i) -> p c t i", i=LINE),
+            )
+
+        def round_whole_list(d):
+            nc.vector.tensor_copy(
+                out=all_rounded[:, d].rearrange("p a (c i t) -> p (a c) t i", i=LINE, t=PACK),
+                in_=fetched[d][:].rearrange("p t (c i) -> p c t i", i=LINE),
             )
 
         z_bf = [[tile("z_bf%d%d" % (a, kind), [P, HALF * PACK], BF16) for kind in range(3)] for a in range(2)]
@@ -278,13 +284,13 @@ def tile_picked_pna_none_po_kernel(
         both = (0, 1)
         for d in range(LISTS):
             fetch_on_vector(0, d, both)
-        for d in range(LISTS):
+        for d, (t, scalar_list) in enumerate(((2, 0), (3, 0), (2, 1))):
             fetch_on_vector(1, d, both)
-            fetch_on_scalar(2 + d % 2, d // 2, both)
-        fetch_on_vector(2, LISTS - 1, (0,))
-        fetch_on_scalar(PACK - 1, 1, both)
-        fetch_on_scalar(PACK - 1, LISTS - 1, both)
-        fetch_on_scalar(2, LISTS - 1, (1,))
+            fetch_on_scalar(t, scalar_list, both)
+        fetch_on_vector(3, 1, both)
+        for a in range(2):
+            fetch_on_scalar(2, LISTS - 1, (a,))
+            fetch_on_scalar(PACK - 1, LISTS - 1, (a,))
         round_mean(0)
         round_mean(1)
         lay_mean(0)
@@ -292,9 +298,8 @@ def tile_picked_pna_none_po_kernel(
         acc_first = [bank(number, "y_acc0%d" % number) for number in (0, 1)]
         acc_second = [bank(number, "y_acc1%d" % number) for number in (2, 3, 4, 5)]
         kinds = (LARGEST, SMALLEST, MEAN)
-        for a in range(2):
-            for d in range(LISTS - 1):
-                round_list(nc.vector.tensor_copy, a, d)
+        for d in range(LISTS - 1):
+            round_whole_list(d)
         round_list(nc.vector.tensor_copy, 0, LISTS - 1)
         extreme_of_two(0, LARGEST)
         extreme_of_two(0, SMALLEST)

@@ -240,7 +240,7 @@ def tile_picked_pna_none_po_kernel(
 
         def second_product(a, kind, acc, kinds):
             per_bank = PACK // len(acc)
-            after = ("z_bf0%d" % SMALLEST, "of_two1%d" % LARGEST)[a] if kind == MEAN else ""
+            after = "z_bf0%d" % (SMALLEST, MEAN)[a] if kind == MEAN else ""
             z_codes = tile("z_codes%d%d" % (a, kind), [P, HALF], U32, after)
             z_plane = tile("z_plane%d%d" % (a, kind), [P, HALF], U8)
             nc.vector.quantize_mx(out=z_codes[:].bitcast(FP8X4), scales=z_plane[:], in_=z_bf[a][kind][:])
@@ -314,8 +314,8 @@ def tile_picked_pna_none_po_kernel(
         extreme_of_three(1, LARGEST)
         kinds = (MEAN, LARGEST, SMALLEST)
         second_product(1, MEAN, acc_second, kinds)
-        second_product(1, LARGEST, acc_second, kinds)
         extreme_of_three(1, SMALLEST)
+        second_product(1, LARGEST, acc_second, kinds)
         second_product(1, SMALLEST, acc_second, kinds)
 
         y_first = store_values(0, acc_first, [nc.scalar.copy] * 2)

@@ -179,15 +179,15 @@ def tile_picked_pna_none_po_kernel(
                 is_transpose=True, start=(t, d) == (0, 0), stop=(t, d) == (PACK - 1, LISTS - 1),
             )
 
-        def fetch_on_vector(t, d, halves):
-            first, last = HALF * halves[0], HALF * (halves[-1] + 1)
+        def fetch_on_vector(t, d, halves, count=V):
+            first, last = HALF * halves[0], min(count, HALF * (halves[-1] + 1))
             offsets = pos_sb[d][:, first // 16 : last // 16]
             nc.vector.tensor_copy(out=fetched[d][:, t, first:last], in_=h[t][:].indirect(offsets))
-            for a in halves:
+            for a in range(halves[0], last // HALF):
                 add_turned(a, t, d)
 
-        def fetch_on_scalar(t, d, halves):
-            first, last = HALF * halves[0], HALF * (halves[-1] + 1)
+        def fetch_on_scalar(t, d, halves, skip=0):
+            first, last = HALF * halves[0] + skip, HALF * (halves[-1] + 1)
             offsets = pos_sb[d][:, first // 16 : last // 16]
             nc.scalar.activation(out=fetched[d][:, t, first:last], in_=h[t][:].indirect(offsets), func=COPY)
             for a in halves:
@@ -240,7 +240,7 @@ def tile_picked_pna_none_po_kernel(
 
         def second_product(a, kind, acc, kinds):
             per_bank = PACK // len(acc)
-            after = "z_bf0%d" % (SMALLEST, MEAN)[a] if kind == MEAN else ""
+            after = ("of_two0%d" % SMALLEST, "fetched%d" % (LISTS - 1))[a] if kind == MEAN else ""
             z_codes = tile("z_codes%d%d" % (a, kind), [P, HALF], U32, after)
             z_plane = tile("z_plane%d%d" % (a, kind), [P, HALF], U8)
             nc.vector.quantize_mx(out=z_codes[:].bitcast(FP8X4), scales=z_plane[:], in_=z_bf[a][kind][:])
@@ -266,18 +266,22 @@ def tile_picked_pna_none_po_kernel(
             nc.sync.dma_start(out=out_rows[:, :, half_of_targets(a)], in_=y[:])
             return y
 
-        def store_codes(a, y, after):
+        def store_codes(a, y, after, copies):
+            width = HALF // len(copies)
+            pieces = [tile("y_bf%d%d" % (a, n), [P, width, PACK], BF16, after) for n in range(len(copies))]
+            for n, copy in enumerate(copies):
+                copy(
+                    out=pieces[n][:].rearrange("p (c i) t -> p c t i", i=LINE),
+                    in_=y[:, :, width * n : width * (n + 1)].rearrange("p t (c i) -> p c t i", i=LINE),
+                )
+            for n, y_bf in enumerate(pieces):
+                cols = slice(HALF * a + width * n, HALF * a + width * (n + 1))
+                nc.vector.quantize_mx(
+                    out=y_codes[:, cols].bitcast(FP8X4),
+                    scales=y_plane[:, cols],
+                    in_=y_bf[:].rearrange("p v t -> p (v t)"),
+                )
             targets = half_of_targets(a)
-            y_bf = tile("y_bf%d" % a, [P, HALF, PACK], BF16, after)
-            nc.vector.tensor_copy(
-                out=y_bf[:].rearrange("p (c i) t -> p c t i", i=LINE),
-                in_=y[:].rearrange("p t (c i) -> p c t i", i=LINE),
-            )
-            nc.vector.quantize_mx(
-                out=y_codes[:, targets].bitcast(FP8X4),
-                scales=y_plane[:, targets],
-                in_=y_bf[:].rearrange("p v t -> p (v t)"),
-            )
             nc.sync.dma_start(out=out_words[:, targets], in_=y_codes[:, targets].bitcast(I32))
 
         deal_weights()
@@ -285,10 +289,12 @@ def tile_picked_pna_none_po_kernel(
         for d in range(LISTS):
             fetch_on_vector(0, d, both)
         for d, (t, scalar_list) in enumerate(((2, 0), (3, 0), (2, 1))):
-            fetch_on_vector(1, d, both)
+            fetch_on_vector(1, d, both, V if d < LISTS - 1 else V - HALF // 2)
             fetch_on_scalar(t, scalar_list, both)
         fetch_on_vector(3, 1, both)
         for a in range(2):
+            if a:
+                fetch_on_scalar(1, LISTS - 1, (a,), HALF // 2)
             fetch_on_scalar(2, LISTS - 1, (a,))
             fetch_on_scalar(PACK - 1, LISTS - 1, (a,))
         round_mean(0)
@@ -319,9 +325,9 @@ def tile_picked_pna_none_po_kernel(
         second_product(1, SMALLEST, acc_second, kinds)
 
         y_first = store_values(0, acc_first, [nc.scalar.copy] * 2)
-        store_codes(0, y_first, "z_bf%d%d" % (1, SMALLEST))
+        store_codes(0, y_first, "z_bf%d%d" % (1, SMALLEST), [nc.vector.tensor_copy])
         y_second = store_values(1, acc_second, [nc.vector.tensor_copy, nc.scalar.copy] * 2)
-        store_codes(1, y_second, "")
+        store_codes(1, y_second, "", [nc.vector.tensor_copy] * 2)
         for q in range(4):
             queue = nc.scalar if q % 2 else nc.sync
             queue.dma_start(

@@ -166,7 +166,7 @@ def tile_picked_pna_none_po_kernel(
                 in_=w_plane[:].rearrange("p (m t) -> p t m", t=PACK),
             )
 
-        fetched = [tile("fetched%d" % d, [P, PACK, V], F32) for d in range(LISTS)]
+        fetched = [tile("fetched%d" % d, [P, PACK, V], F32, "xp_codes" if d == LISTS - 1 else "") for d in range(LISTS)]
         all_rounded = tile("all_rounded", [P, LISTS, 2, HALF * PACK], BF16, "w_codes")
         rounded = [[all_rounded[:, d, a] for d in range(LISTS)] for a in range(2)]
         of_two = [{kind: tile("of_two%d%d" % (a, kind), [P, HALF * PACK], BF16) for kind in EXTREME_OP} for a in range(2)]
@@ -179,19 +179,20 @@ def tile_picked_pna_none_po_kernel(
                 is_transpose=True, start=(t, d) == (0, 0), stop=(t, d) == (PACK - 1, LISTS - 1),
             )
 
-        def fetch_on_vector(t, d, halves, count=V):
-            first, last = HALF * halves[0], min(count, HALF * (halves[-1] + 1))
+        def turn_complete_halves(t, d, first, last):
+            for a in range(2):
+                if first < HALF * (a + 1) <= last:
+                    add_turned(a, t, d)
+
+        def fetch_on_vector(t, d, first=0, last=V):
             offsets = pos_sb[d][:, first // 16 : last // 16]
             nc.vector.tensor_copy(out=fetched[d][:, t, first:last], in_=h[t][:].indirect(offsets))
-            for a in range(halves[0], last // HALF):
-                add_turned(a, t, d)
+            turn_complete_halves(t, d, first, last)
 
-        def fetch_on_scalar(t, d, halves, skip=0):
-            first, last = HALF * halves[0] + skip, HALF * (halves[-1] + 1)
+        def fetch_on_scalar(t, d, first=0, last=V):
             offsets = pos_sb[d][:, first // 16 : last // 16]
             nc.scalar.activation(out=fetched[d][:, t, first:last], in_=h[t][:].indirect(offsets), func=COPY)
-            for a in halves:
-                add_turned(a, t, d)
+            turn_complete_halves(t, d, first, last)
 
         def round_mean(a):
             turned = tile("turned%d" % a, [P, 2, P, 2], BF16)
@@ -240,7 +241,7 @@ def tile_picked_pna_none_po_kernel(
 
         def second_product(a, kind, acc, kinds):
             per_bank = PACK // len(acc)
-            after = ("of_two0%d" % SMALLEST, "fetched%d" % (LISTS - 1))[a] if kind == MEAN else ""
+            after = ("of_two0%d" % SMALLEST, "xp_codes")[a] if kind == MEAN else ""
             z_codes = tile("z_codes%d%d" % (a, kind), [P, HALF], U32, after)
             z_plane = tile("z_plane%d%d" % (a, kind), [P, HALF], U8)
             nc.vector.quantize_mx(out=z_codes[:].bitcast(FP8X4), scales=z_plane[:], in_=z_bf[a][kind][:])
@@ -285,18 +286,21 @@ def tile_picked_pna_none_po_kernel(
             nc.sync.dma_start(out=out_words[:, targets], in_=y_codes[:, targets].bitcast(I32))
 
         deal_weights()
-        both = (0, 1)
-        for d in range(LISTS):
-            fetch_on_vector(0, d, both)
-        for d, (t, scalar_list) in enumerate(((2, 0), (3, 0), (2, 1))):
-            fetch_on_vector(1, d, both, V if d < LISTS - 1 else V - HALF // 2)
-            fetch_on_scalar(t, scalar_list, both)
-        fetch_on_vector(3, 1, both)
-        for a in range(2):
-            if a:
-                fetch_on_scalar(1, LISTS - 1, (a,), HALF // 2)
-            fetch_on_scalar(2, LISTS - 1, (a,))
-            fetch_on_scalar(PACK - 1, LISTS - 1, (a,))
+        last_list = LISTS - 1
+        fetch_on_vector(0, 0)
+        fetch_on_vector(0, 1)
+        fetch_on_scalar(2, 0)
+        fetch_on_vector(1, 0)
+        fetch_on_vector(1, 1)
+        fetch_on_scalar(1, last_list, 0, HALF)
+        fetch_on_vector(2, 1)
+        fetch_on_scalar(3, 0)
+        fetch_on_vector(0, last_list, 0, HALF)
+        fetch_on_scalar(2, last_list, 0, HALF)
+        fetch_on_vector(3, 1)
+        fetch_on_scalar(3, last_list, 0, HALF)
+        for t in range(PACK):
+            fetch_on_scalar(t, last_list, HALF, V)
         round_mean(0)
         round_mean(1)
         lay_mean(0)

from contextlib import ExitStack

import concourse.mybir as mybir
from concourse.masks import make_identity

K, T, S, V, H = 512, 1024, 512, 256, 512
FLOPS = 2 * K * H * S + 3 * 2 * H * H * V

F32 = mybir.dt.float32
BF16 = mybir.dt.bfloat16
I32 = mybir.dt.int32
U32 = mybir.dt.uint32
U16 = mybir.dt.uint16
U8 = mybir.dt.uint8
FP8X4 = mybir.dt.float8_e4m3fn_x4
ALU = mybir.AluOpType
COPY = mybir.ActivationFunctionType.Copy

P = 128
PACK = 4
LISTS = 3
HALF = V // 2
LINE = 4
PARTS = ((0, 256), (256, 128), (384, 128))
MEAN, LARGEST, SMALLEST = 0, 1, 2
EXTREME_OP = {LARGEST: ALU.max, SMALLEST: ALU.min}


def as_words(words):
    return words[0].rearrange("p n r -> p (n r)").bitcast(I32)


def load_scale_rows(nc, plane, first_row, scales):
    for q in range(4):
        row = 32 * q + first_row
        nc.sync.dma_start(out=plane[row : row + 4, :].bitcast(I32), in_=scales[0, 4 * q : 4 * q + 4, :].bitcast(I32))


def half_of_targets(a):
    return slice(HALF * a, HALF * (a + 1))


def tile_picked_pna_none_po_kernel(
    tc, x_words, x_scales, w1, w2_words, w2_scales, w3_words, w3_scales, w4_words, w4_scales,
    offs, pos1, pos2, pos3, out_0, out_1, out_2,
):
    nc = tc.nc
    with ExitStack() as ctx:
        sb = ctx.enter_context(tc.tile_pool(name="sb", bufs=1))
        ps = ctx.enter_context(tc.psum_pool(name="ps", bufs=1))

        def tile(name, shape, dtype, after=""):
            return sb.tile(shape, dtype, name=name, tag=after or name, align_bytes=64)

        def bank(number, name):
            return ps.tile([P, 512], F32, name=name, tag="bank%d" % number)

        offs_sb = tile("offs_sb", [P, S // 16], U16)
        pos_sb = [tile("pos_sb%d" % d, [P, V // 16], U16) for d in range(LISTS)]
        x_plane = tile("x_plane", [P, T], U8)
        x_codes = tile("x_codes", [P, T], U32)
        w1_raw = tile("w1_raw", [P, PACK, H], F32)
        w_codes = tile("w_codes", [P, 3, H], U32)
        w_plane = tile("w_plane", [P, H], U8)
        identity = tile("identity", [P, P], F32)

        nc.gpsimd.memset(x_plane[:].bitcast(I32), 0)
        nc.gpsimd.memset(w_plane[:].bitcast(I32), 0)
        make_identity(nc, identity[:])

        w1_rows = w1.rearrange("(p j) c -> p j c", j=PACK)
        nc.sync.dma_start(out=w1_raw[:, 0:2, :], in_=w1_rows[:, 0:2, :])
        nc.sync.dma_start(out=offs_sb[:], in_=offs)
        load_scale_rows(nc, x_plane, 0, x_scales)
        nc.sync.dma_start(out=w1_raw[:, 2:4, :], in_=w1_rows[:, 2:4, :])
        nc.sync.dma_start(out=x_codes[:].bitcast(I32), in_=as_words(x_words))
        for d, pos in enumerate((pos1, pos2, pos3)):
            nc.sync.dma_start(out=pos_sb[d][:], in_=pos)
        for kind, words in enumerate((w2_words, w3_words, w4_words)):
            nc.sync.dma_start(out=w_codes[:, kind, :].bitcast(I32), in_=as_words(words))
        for kind, scales in enumerate((w2_scales, w3_scales, w4_scales)):
            load_scale_rows(nc, w_plane, 4 * kind, scales)

        xp_plane = tile("xp_plane", [P, S], U8)
        xp_codes = tile("xp_codes", [P, S], U32)
        w1_bf = tile("w1_bf", [P, PACK, P, PACK], BF16)
        early_codes = tile("early_codes", [P, H // 2], U32)
        later_codes = tile("later_codes", [P, H // 2], U32, "x_codes")
        w1_codes = [(early_codes, later_codes)[t // 2][:, P * (t % 2) : P * (t % 2 + 1)] for t in range(PACK)]
        w1_plane = tile("w1_plane", [P, H], U8)

        def w1_views(t0, t1, j0=0, j1=PACK):
            dst = w1_bf[:, t0:t1, :, j0:j1].rearrange("p t m j -> p m t j")
            src = w1_raw[:, j0:j1, :].rearrange("p j (m t) -> p m t j", t=PACK)[:, :, t0:t1, :]
            return dst, src

        def quantise_w1(t):
            cols = slice(P * t, P * (t + 1))
            nc.vector.quantize_mx(
                out=w1_codes[t].bitcast(FP8X4),
                scales=w1_plane[:, cols],
                in_=w1_bf[:, t].rearrange("p m j -> p (m j)"),
            )

        def first_pass(t, out, first, count):
            cols = slice(P * t, P * (t + 1))
            nc.tensor.matmul_mx(
                out=out,
                lhsT=w1_codes[t].bitcast(FP8X4),
                lhsT_scale=w1_plane[:, cols],
                rhs=xp_codes[:, first : first + count].bitcast(FP8X4),
                rhs_scale=xp_plane[:, first : first + count],
                start=True,
                stop=True,
            )

        dst, src = w1_views(1, PACK, 0, 2)
        nc.scalar.activation(out=dst, in_=src, func=COPY)
        dst, src = w1_views(0, 1, 0, 2)
        nc.vector.tensor_copy(out=dst, in_=src)
        nc.vector.tensor_copy(out=xp_plane[:], in_=x_plane[:].indirect(offs_sb[:]))
        dst, src = w1_views(0, 1, 2, PACK)
        nc.vector.tensor_copy(out=dst, in_=src)
        dst, src = w1_views(1, 2, 2, PACK)
        nc.scalar.copy(out=dst, in_=src)
        dst, src = w1_views(2, PACK, 2, PACK)
        nc.scalar.copy(out=dst, in_=src)
        quantise_w1(0)
        quantise_w1(1)

        h = [tile("h%d" % t, [P, S], F32) for t in range(PACK)]
        acc1 = bank(1, "h_acc1")
        for part, (first, count) in enumerate(PARTS):
            nc.vector.tensor_copy(
                out=xp_codes[:, first : first + count],
                in_=x_codes[:].indirect(offs_sb[:, first // 16 : (first + count) // 16]),
            )
            acc = bank((0, 7, 6)[part], "h_acc0%d" % part)
            first_pass(0, acc[:, 0:count], first, count)
            if part == 0:
                first_pass(1, acc1[:, 0:count], first, count)
            nc.scalar.copy(out=h[0][:, first : first + count], in_=acc[:, 0:count])
        quantise_w1(2)
        quantise_w1(3)
        first_pass(1, acc1[:, S // 2 : S], S // 2, S // 2)
        nc.scalar.copy(out=h[1][:], in_=acc1[:])
        for t in range(2, PACK):
            acc = bank(t, "h_acc%d" % t)
            first_pass(t, acc[:], 0, S)
            nc.scalar.copy(out=h[t][:], in_=acc[:])

        wd_codes = tile("wd_codes", [P, 3, H], U32, "w1_bf")
        wd_plane = tile("wd_plane", [P, H], U8)
        y_codes = tile("y_codes", [P, V], U32)
        y_plane = tile("y_plane", [P, V], U8)
        out_rows = out_0.rearrange("(p t) v -> p t v", t=PACK)
        out_words = as_words(out_1)

        def deal_weights():
            nc.gpsimd.tensor_copy(
                out=wd_codes[:].bitcast(I32).rearrange("p k (t m) -> p k t m", t=PACK),
                in_=w_codes[:].bitcast(I32).rearrange("p k (m t) -> p k t m", t=PACK),
            )
            nc.gpsimd.tensor_copy(
                out=wd_plane[:].rearrange("p (t m) -> p t m", t=PACK),
                in_=w_plane[:].rearrange("p (m t) -> p t m", t=PACK),
            )

        fetched = [tile("fetched%d" % d, [P, PACK, V], F32, "xp_codes" if d == LISTS - 1 else "") for d in range(LISTS)]
        all_rounded = tile("all_rounded", [P, LISTS, 2, HALF * PACK], BF16, "w_codes")
        rounded = [[all_rounded[:, d, a] for d in range(LISTS)] for a in range(2)]
        of_two = [{kind: tile("of_two%d%d" % (a, kind), [P, HALF * PACK], BF16) for kind in EXTREME_OP} for a in range(2)]
        sums = [bank(4 + a, "sums%d" % a) for a in range(2)]
        mean_back = [bank(6 + a, "mean_back%d" % a) for a in range(2)]

        def add_turned(a, t, d):
            nc.tensor.matmul(
                out=sums[a][:, P * t : P * (t + 1)], lhsT=fetched[d][:, t, half_of_targets(a)], rhs=identity[:],
                is_transpose=True, start=(t, d) == (0, 0), stop=(t, d) == (PACK - 1, LISTS - 1),
            )

        def turn_complete_halves(t, d, first, last):
            for a in range(2):
                if first < HALF * (a + 1) <= last:
                    add_turned(a, t, d)

        def fetch_on_vector(t, d, first=0, last=V):
            offsets = pos_sb[d][:, first // 16 : last // 16]
            nc.vector.tensor_copy(out=fetched[d][:, t, first:last], in_=h[t][:].indirect(offsets))
            turn_complete_halves(t, d, first, last)

        def fetch_on_scalar(t, d, first=0, last=V):
            offsets = pos_sb[d][:, first // 16 : last // 16]
            nc.scalar.activation(out=fetched[d][:, t, first:last], in_=h[t][:].indirect(offsets), func=COPY)
            turn_complete_halves(t, d, first, last)

        def round_mean(a):
            turned = tile("turned%d" % a, [P, 2, P, 2], BF16)
            nc.scalar.activation(
                out=turned[:],
                in_=sums[a][:].rearrange("v (u e p) -> v u p e", u=2, e=2),
                func=COPY,
                scale=1.0 / LISTS,
            )
            for u in range(2):
                nc.tensor.transpose(
                    mean_back[a][:, P * u : P * (u + 1)],
                    turned[:, u].rearrange("v p e -> v (p e)").bitcast(F32),
                    identity[:],
                )

        def round_list(copy, a, d):
            copy(
                out=rounded[a][d].rearrange("p (c i t) -> p c t i", i=LINE, t=PACK),
                in_=fetched[d][:, :, half_of_targets(a)].rearrange("p t (c i) -> p c t i", i=LINE),
            )

        def round_whole_list(d):
            nc.vector.tensor_copy(
                out=all_rounded[:, d].rearrange("p a (c i t) -> p (a c) t i", i=LINE, t=PACK),
                in_=fetched[d][:].rearrange("p t (c i) -> p c t i", i=LINE),
            )

        z_bf = [[tile("z_bf%d%d" % (a, kind), [P, HALF * PACK], BF16) for kind in range(3)] for a in range(2)]

        def lay_mean(a):
            nc.scalar.copy(
                out=z_bf[a][MEAN][:].bitcast(F32).rearrange("p (v u) -> p v u", u=2),
                in_=mean_back[a][:, 0 : 2 * P].rearrange("p (u v) -> p v u", u=2),
            )

        def extreme_of_two(a, kind):
            nc.vector.tensor_tensor(
                out=of_two[a][kind][:], in0=rounded[a][0], in1=rounded[a][1], op=EXTREME_OP[kind]
            )

        def extreme_of_three(a, kind):
            nc.vector.tensor_tensor(
                out=z_bf[a][kind][:], in0=of_two[a][kind][:], in1=rounded[a][2], op=EXTREME_OP[kind]
            )

        def second_product(a, kind, acc, kinds):
            per_bank = PACK // len(acc)
            after = ("of_two0%d" % SMALLEST, "xp_codes")[a] if kind == MEAN else ""
            z_codes = tile("z_codes%d%d" % (a, kind), [P, HALF], U32, after)
            z_plane = tile("z_plane%d%d" % (a, kind), [P, HALF], U8)
            nc.vector.quantize_mx(out=z_codes[:].bitcast(FP8X4), scales=z_plane[:], in_=z_bf[a][kind][:])
            for t in range(PACK):
                cols = slice(P * t, P * (t + 1))
                place = t % per_bank
                nc.tensor.matmul_mx(
                    out=acc[t // per_bank][:, HALF * place : HALF * (place + 1)],
                    lhsT=wd_codes[:, kind, cols].bitcast(FP8X4),
                    lhsT_scale=wd_plane[4 * kind : P, cols],
                    rhs=z_codes[:].bitcast(FP8X4),
                    rhs_scale=z_plane[:],
                    start=(kind == kinds[0] and place == 0),
                    stop=(kind == kinds[-1] and place == per_bank - 1),
                )

        def store_values(a, acc, copies):
            y = tile("y%d" % a, [P, PACK, HALF], F32)
            y_flat = y[:].rearrange("p t v -> p (t v)")
            width = PACK * HALF // len(acc)
            for n, copy in enumerate(copies):
                copy(out=y_flat[:, width * n : width * (n + 1)], in_=acc[n][:, 0:width])
            nc.sync.dma_start(out=out_rows[:, :, half_of_targets(a)], in_=y[:])
            return y

        def store_codes(a, y, after, copies):
            width = HALF // len(copies)
            pieces = [tile("y_bf%d%d" % (a, n), [P, width, PACK], BF16, after) for n in range(len(copies))]
            for n, copy in enumerate(copies):
                copy(
                    out=pieces[n][:].rearrange("p (c i) t -> p c t i", i=LINE),
                    in_=y[:, :, width * n : width * (n + 1)].rearrange("p t (c i) -> p c t i", i=LINE),
                )
            for n, y_bf in enumerate(pieces):
                cols = slice(HALF * a + width * n, HALF * a + width * (n + 1))
                nc.vector.quantize_mx(
                    out=y_codes[:, cols].bitcast(FP8X4),
                    scales=y_plane[:, cols],
                    in_=y_bf[:].rearrange("p v t -> p (v t)"),
                )
            targets = half_of_targets(a)
            nc.sync.dma_start(out=out_words[:, targets], in_=y_codes[:, targets].bitcast(I32))

        deal_weights()
        last_list = LISTS - 1
        fetch_on_vector(0, 0)
        fetch_on_vector(0, 1)
        fetch_on_scalar(2, 0)
        fetch_on_vector(1, 0)
        fetch_on_vector(1, 1)
        fetch_on_scalar(1, last_list, 0, HALF)
        fetch_on_vector(2, 1)
        fetch_on_scalar(3, 0)
        fetch_on_vector(0, last_list, 0, HALF)
        fetch_on_scalar(2, last_list, 0, HALF)
        fetch_on_vector(3, 1)
        fetch_on_scalar(3, last_list, 0, HALF)
        for t in range(PACK):
            fetch_on_scalar(t, last_list, HALF, V)
        round_mean(0)
        round_mean(1)
        lay_mean(0)
        lay_mean(1)
        acc_first = [bank(number, "y_acc0%d" % number) for number in (0, 1)]
        acc_second = [bank(number, "y_acc1%d" % number) for number in (2, 3, 4, 5)]
        kinds = (LARGEST, SMALLEST, MEAN)
        for d in range(LISTS - 1):
            round_whole_list(d)
        round_list(nc.vector.tensor_copy, 0, LISTS - 1)
        extreme_of_two(0, LARGEST)
        extreme_of_two(0, SMALLEST)
        extreme_of_three(0, LARGEST)
        extreme_of_three(0, SMALLEST)
        second_product(0, LARGEST, acc_first, kinds)
        second_product(0, SMALLEST, acc_first, kinds)
        extreme_of_two(1, LARGEST)
        round_list(nc.vector.tensor_copy, 1, LISTS - 1)
        second_product(0, MEAN, acc_first, kinds)
        extreme_of_two(1, SMALLEST)
        extreme_of_three(1, LARGEST)
        kinds = (MEAN, LARGEST, SMALLEST)
        second_product(1, MEAN, acc_second, kinds)
        extreme_of_three(1, SMALLEST)
        second_product(1, LARGEST, acc_second, kinds)
        second_product(1, SMALLEST, acc_second, kinds)

        y_first = store_values(0, acc_first, [nc.scalar.copy] * 2)
        store_codes(0, y_first, "z_bf%d%d" % (1, SMALLEST), [nc.vector.tensor_copy])
        y_second = store_values(1, acc_second, [nc.vector.tensor_copy, nc.scalar.copy] * 2)
        store_codes(1, y_second, "", [nc.vector.tensor_copy] * 2)
        for q in range(4):
            queue = nc.scalar if q % 2 else nc.sync
            queue.dma_start(
                out=out_2[0, 4 * q : 4 * q + 4, :].bitcast(I32),
                in_=y_plane[32 * q : 32 * q + 4, :].bitcast(I32),
            )
